import numpy as np
import ml_dtypes


def mxq(x, axis, fmt="e4m3"):
    dtype, down = {"e4m3": (ml_dtypes.float8_e4m3fn, 7), "e5m2": (ml_dtypes.float8_e5m2, 14)}[fmt]
    v = np.moveaxis(np.asarray(x, np.float32).astype(ml_dtypes.bfloat16).astype(np.float64), axis, -1)
    blocks = v.reshape(v.shape[:-1] + (-1, 32))
    amax = np.abs(blocks).max(-1, keepdims=True)
    byte = np.maximum(np.where(amax > 0, np.frexp(amax)[1] - 1 + 127, 0) - down, 1)
    scale = np.exp2(byte - 127.0)
    codes = (blocks / scale).astype(np.float32).astype(dtype).astype(np.float64)
    return np.moveaxis((codes * scale).reshape(v.shape), -1, axis)


WIDE = False


def mx_kscale(k):
    if not WIDE:
        return np.ones(k)
    levels = np.array([10, -10, 5, -5, 0])
    if k % 512:
        return np.exp2(np.random.permutation(np.resize(levels, k // 32))).repeat(32)
    a = np.empty((k // 512, 16))
    for p in range(k // 512):
        a[p, :8] = np.random.permutation(np.resize(levels, 8))
        for g in range(8):
            far = levels[np.abs(levels - a[p, g]) >= 10]
            a[p, g + 8] = far[np.random.randint(len(far))]
    return np.exp2(a.ravel()).repeat(32)


def f64(x):
    return np.asarray(x).astype(np.float64)


def striped(idx):
    return np.tile(idx.reshape(-1, 16).T, (8, 1)).astype(np.uint16)


def unstriped(offs):
    return offs[:16].T.reshape(-1).astype(np.int64)


def pack_weight(w):
    k, n = w.shape
    w = f64(np.asarray(w, np.float32).astype(ml_dtypes.bfloat16)).reshape(k // 32, 32, n)
    amax = np.abs(w).max(1)
    byte = np.clip(np.where(amax > 0, np.frexp(amax)[1] - 1 + 127 - 7, 1), 1, 254)
    scaled = (w * np.exp2(127.0 - byte)[:, None, :]).reshape(k, n).astype(np.float32)
    words = np.ascontiguousarray(scaled.reshape(k // 512, 128, 4, n).transpose(0, 1, 3, 2)).astype(ml_dtypes.float8_e4m3fn).view(np.uint8)
    return words, np.ascontiguousarray(byte.astype(np.uint8).reshape(k // 512, 16, n))


def unpack_weight(words, scales):
    g, p, n, _ = words.shape
    vals = np.ascontiguousarray(words).view(ml_dtypes.float8_e4m3fn).astype(np.float64) * np.repeat(np.exp2(scales.astype(np.float64) - 127.0), 8, axis=1)[..., None]
    return vals.transpose(0, 1, 3, 2).reshape(g * 512, n)


def relu(v):
    return np.maximum(v, 0.0)


K, T, S, V, U, D = 512, 1024, 512, 512, 256, 4
P = 2 ** 7


def setup_inputs():
    n = np.random.standard_normal
    s = mx_kscale(K)[:, None]
    near = np.random.permutation(S)
    packed_xT = pack_weight(n((K, T)) * s)
    return {
        "x_words": packed_xT[0],
        "x_scales": packed_xT[1],
        "hT": (n((K, V)) / np.sqrt(K) / s).astype(np.float32),
        "bias": (np.tile(0.3 * n(T), (P, 1))).astype(np.float32),
        "code": (np.tile(np.where(np.random.uniform(size=(D, 1, U)) < 0.5, 1.0, -1.0), (1, P, 1))).astype(np.float32),
        "offs": striped(np.random.permutation(T)[:S]),
        "pos1": striped(near[:U]),
        "pos2": striped(near[U:]),
        "pos3": striped(np.random.permutation(S)[:U]),
        "pos4": striped(np.random.permutation(S)[:U]),
    }


def reference(x_words, x_scales, hT, bias, code, offs, pos1, pos2, pos3, pos4):
    hTq = mxq(f64(hT), 0, "e4m3")
    xq = unpack_weight(x_words, x_scales)[:, unstriped(offs)]
    y = (hTq.T @ xq) + f64(bias)[:1][:, unstriped(offs)]
    return (relu(-1.0 * (y[:, unstriped(pos1)] * f64(code)[0, :1]) + 1.0) + relu(-1.0 * (y[:, unstriped(pos2)] * f64(code)[1, :1]) + 1.0) + relu(-1.0 * (y[:, unstriped(pos3)] * f64(code)[2, :1]) + 1.0) + relu(-1.0 * (y[:, unstriped(pos4)] * f64(code)[3, :1]) + 1.0)) / 4

@@ -1,0 +1,162 @@
+from contextlib import ExitStack
+
+import concourse.mybir as mybir
+from concourse.masks import make_identity
+
+K, T, S, V, U, D = 512, 1024, 512, 512, 256, 4
+FLOPS = 2 * K * V * S
+
+F32 = mybir.dt.float32
+BF16 = mybir.dt.bfloat16
+I32 = mybir.dt.int32
+U32 = mybir.dt.uint32
+U16 = mybir.dt.uint16
+U8 = mybir.dt.uint8
+FP8X4 = mybir.dt.float8_e4m3fn_x4
+ALU = mybir.AluOpType
+ACT = mybir.ActivationFunctionType
+
+P = 128
+PACK = 4
+BLOCKS = V // P
+HALVES = U // P
+LATE = 2
+H_PIECES = ((0, 128), (128, 256), (256, 512))
+
+
+def tile_picked_yecoc_sum_p_kernel(
+    tc, x_words, x_scales, hT, bias, code, offs, pos1, pos2, pos3, pos4, out
+):
+    nc = tc.nc
+    with ExitStack() as ctx:
+        keep = ctx.enter_context(tc.tile_pool(name="keep", bufs=1))
+        psum = ctx.enter_context(tc.psum_pool(name="psum", bufs=1))
+
+        offs_sb = keep.tile([P, S // 16], U16, name="offs_sb")
+        nc.sync.dma_start(offs_sb[:], offs)
+
+        scale_table = keep.tile([P, T], U8, name="scale_table")
+        nc.vector.memset(scale_table[:].bitcast(I32), 0)
+        for q in range(4):
+            nc.scalar.dma_start(
+                scale_table[32 * q : 32 * q + 4, :].bitcast(I32), x_scales[0, 4 * q : 4 * q + 4, :].bitcast(I32)
+            )
+
+        word_table = keep.tile([P, T], U32, name="word_table")
+        nc.sync.dma_start(word_table[:].bitcast(I32), x_words[0].rearrange("p n t -> p (n t)").bitcast(I32))
+
+        h_rows = hT.rearrange("(p j) w -> p j w", j=PACK)
+        h_raw = [keep.tile([P, PACK, hi - lo], F32, name="h_raw%d" % lo) for lo, hi in H_PIECES]
+        nc.sync.dma_start(h_raw[0][:], h_rows[:, :, 0:128])
+
+        bias_table = keep.tile([P, T], F32, name="bias_table")
+        nc.sync.dma_start(bias_table[:], bias)
+
+        pos_sb = []
+        for d, pos in enumerate((pos1, pos2, pos3, pos4)):
+            lst = keep.tile([P, U // 16], U16, name="pos_sb%d" % d)
+            nc.sync.dma_start(lst[:], pos)
+            pos_sb.append(lst)
+
+        code_sb = keep.tile([P, D, U], F32, name="code_sb")
+        nc.sync.dma_start(code_sb[:], code.rearrange("d p r -> p d r"))
+        for i in (1, 2):
+            lo, hi = H_PIECES[i]
+            nc.sync.dma_start(h_raw[i][:], h_rows[:, :, lo:hi])
+
+        ident = keep.tile([P, P], F32, name="ident")
+        make_identity(nc, ident[:])
+
+        x_scale = keep.tile([P, S], U8, name="x_scale", align_bytes=64)
+        nc.vector.tensor_copy(x_scale[:], scale_table[:].indirect(offs_sb[:]))
+        x_code = keep.tile([P, S], U32, name="x_code", align_bytes=64)
+        nc.vector.tensor_copy(x_code[:], word_table[:].indirect(offs_sb[:]))
+
+        h_code, h_scale = [], []
+
+        def quantise(i):
+            lo, hi = H_PIECES[i]
+            w = hi - lo
+            grouped = keep.tile([P, w, PACK], BF16, name="grouped%d" % i, align_bytes=64)
+            nc.scalar.copy(
+                grouped[:].rearrange("p (c i) t -> p c t i", i=4),
+                h_raw[i][:].rearrange("p t (c i) -> p c t i", i=4),
+            )
+            codes = keep.tile([P, w], U32, name="h_code%d" % i, align_bytes=64)
+            scales = keep.tile([P, w], U8, name="h_scale%d" % i, align_bytes=64)
+            nc.vector.quantize_mx(
+                out=codes[:].bitcast(FP8X4), scales=scales[:], in_=grouped[:].rearrange("p w j -> p (w j)")
+            )
+            for c in range(0, w, P):
+                h_code.append(codes[:, c : c + P])
+                h_scale.append(scales[:, c : c + P])
+
+        quantise(0)
+        bias_picked = keep.tile([P, S], F32, name="bias_picked")
+        nc.vector.tensor_copy(bias_picked[:], bias_table[:].indirect(offs_sb[:]))
+        quantise(1)
+        quantise(2)
+
+        last_code = keep.tile([P, U], F32, name="last_code")
+        nc.scalar.mul(last_code[:], code_sb[:, D - 1, :], -1.0 / D)
+
+        def scores(b):
+            acc = psum.tile([P, S], F32, name="acc", tag="acc", bufs=2)
+            nc.tensor.matmul_mx(
+                out=acc[:],
+                lhsT=h_code[b].bitcast(FP8X4),
+                lhsT_scale=h_scale[b],
+                rhs=x_code[:].bitcast(FP8X4),
+                rhs_scale=x_scale[:],
+                start=True,
+                stop=True,
+            )
+            y = keep.tile([P, S], F32, name="y%d" % b)
+            nc.vector.tensor_tensor(y[:], acc[:], bias_picked[:], ALU.add)
+            return y
+
+        def summed_hinges(b, y, terms, offset):
+            sums = [psum.tile([P, P], F32, name="sum%d" % h, tag="sum%d" % h, bufs=2) for h in range(HALVES)]
+            for d in range(terms):
+                margin = keep.tile([P, U], F32, name="margin%d_%d" % (b, d))
+                nc.vector.tensor_tensor(margin[:], y[:].indirect(pos_sb[d][:]), code_sb[:, d, :], ALU.mult)
+                hinge = keep.tile([P, U], F32, name="hinge%d_%d" % (b, d))
+                nc.scalar.activation(hinge[:], margin[:], ACT.Relu, bias=1.0 / D, scale=-1.0 / D)
+                for h in range(HALVES):
+                    nc.tensor.matmul(
+                        sums[h][:],
+                        hinge[:, h * P : (h + 1) * P],
+                        ident[:],
+                        start=(d == 0),
+                        stop=(d == terms - 1),
+                        is_transpose=True,
+                    )
+            turned = keep.tile([P, HALVES, P], F32, name="turned%d" % b)
+            back = psum.tile([P, U], F32, name="back", tag="back", bufs=2)
+            for h in range(HALVES):
+                nc.scalar.activation(turned[:, h, :], sums[h][:], ACT.Copy, bias=offset)
+                nc.tensor.transpose(back[:, h * P : (h + 1) * P], turned[:, h, :], ident[:])
+            return back
+
+        partial = {}
+        for b in range(BLOCKS):
+            y = scores(b)
+            if b < BLOCKS - LATE:
+                back = summed_hinges(b, y, D, 0.0)
+                result = keep.tile([P, U], F32, name="result%d" % b)
+                nc.scalar.copy(result[:], back[:])
+                nc.sync.dma_start(out[b * P : (b + 1) * P, :], result[:])
+            else:
+                partial[b] = (y, summed_hinges(b, y, D - 1, 1.0 / D))
+        last_margin = {}
+        for b in range(BLOCKS - LATE, BLOCKS):
+            last_margin[b] = keep.tile([P, U], F32, name="last_margin%d" % b)
+            nc.vector.tensor_tensor(
+                last_margin[b][:], partial[b][0][:].indirect(pos_sb[D - 1][:]), last_code[:], ALU.mult
+            )
+        for b in range(BLOCKS - LATE, BLOCKS):
+            result = keep.tile([P, U], F32, name="result%d" % b)
+            nc.vector.scalar_tensor_tensor(
+                result[:], last_margin[b][:], -1.0 / D, partial[b][1][:], ALU.max, ALU.add
+            )
+            nc.sync.dma_start(out[b * P : (b + 1) * P, :], result[:])

@@ -20,8 +20,8 @@ P = 128
 PACK = 4
 BLOCKS = V // P
 HALVES = U // P
-LATE = 2
-H_PIECES = ((0, 128), (128, 256), (256, 512))
+LATE = 3
+PIECE = V // 2
 
 
 def tile_picked_yecoc_sum_p_kernel(
@@ -33,69 +33,60 @@ def tile_picked_yecoc_sum_p_kernel(
         psum = ctx.enter_context(tc.psum_pool(name="psum", bufs=1))
 
         offs_sb = keep.tile([P, S // 16], U16, name="offs_sb")
-        nc.sync.dma_start(offs_sb[:], offs)
-
+        pos_sb = [keep.tile([P, U // 16], U16, name="pos_sb%d" % d) for d in range(D)]
         scale_table = keep.tile([P, T], U8, name="scale_table")
+        word_table = keep.tile([P, T], U32, name="word_table")
+        bias_table = keep.tile([P, T], F32, name="bias_table")
+        code_sb = keep.tile([P, D, U], F32, name="code_sb")
+        h_raw = [keep.tile([P, PACK, PIECE], F32, name="h_raw%d" % i) for i in range(2)]
+        h_rows = hT.rearrange("(p j) w -> p j w", j=PACK)
+
         nc.vector.memset(scale_table[:].bitcast(I32), 0)
+        nc.sync.dma_start(offs_sb[:], offs)
+        nc.sync.dma_start(word_table[:].bitcast(I32), x_words[0].rearrange("p n t -> p (n t)").bitcast(I32))
         for q in range(4):
-            nc.scalar.dma_start(
+            nc.sync.dma_start(
                 scale_table[32 * q : 32 * q + 4, :].bitcast(I32), x_scales[0, 4 * q : 4 * q + 4, :].bitcast(I32)
             )
-
-        word_table = keep.tile([P, T], U32, name="word_table")
-        nc.sync.dma_start(word_table[:].bitcast(I32), x_words[0].rearrange("p n t -> p (n t)").bitcast(I32))
-
-        h_rows = hT.rearrange("(p j) w -> p j w", j=PACK)
-        h_raw = [keep.tile([P, PACK, hi - lo], F32, name="h_raw%d" % lo) for lo, hi in H_PIECES]
-        nc.sync.dma_start(h_raw[0][:], h_rows[:, :, 0:128])
-
-        bias_table = keep.tile([P, T], F32, name="bias_table")
+        nc.sync.dma_start(h_raw[0][:], h_rows[:, :, 0:PIECE])
         nc.sync.dma_start(bias_table[:], bias)
-
-        pos_sb = []
-        for d, pos in enumerate((pos1, pos2, pos3, pos4)):
-            lst = keep.tile([P, U // 16], U16, name="pos_sb%d" % d)
+        nc.sync.dma_start(h_raw[1][:], h_rows[:, :, PIECE:V])
+        for lst, pos in zip(pos_sb, (pos1, pos2, pos3, pos4)):
             nc.sync.dma_start(lst[:], pos)
-            pos_sb.append(lst)
-
-        code_sb = keep.tile([P, D, U], F32, name="code_sb")
         nc.sync.dma_start(code_sb[:], code.rearrange("d p r -> p d r"))
-        for i in (1, 2):
-            lo, hi = H_PIECES[i]
-            nc.sync.dma_start(h_raw[i][:], h_rows[:, :, lo:hi])
 
         ident = keep.tile([P, P], F32, name="ident")
         make_identity(nc, ident[:])
 
-        x_scale = keep.tile([P, S], U8, name="x_scale", align_bytes=64)
-        nc.vector.tensor_copy(x_scale[:], scale_table[:].indirect(offs_sb[:]))
         x_code = keep.tile([P, S], U32, name="x_code", align_bytes=64)
         nc.vector.tensor_copy(x_code[:], word_table[:].indirect(offs_sb[:]))
+        x_scale = keep.tile([P, S], U8, name="x_scale", align_bytes=64)
+        nc.vector.tensor_copy(x_scale[:], scale_table[:].indirect(offs_sb[:]))
 
-        h_code, h_scale = [], []
-
-        def quantise(i):
-            lo, hi = H_PIECES[i]
-            w = hi - lo
-            grouped = keep.tile([P, w, PACK], BF16, name="grouped%d" % i, align_bytes=64)
+        def interleave(i, tag):
+            grouped = keep.tile([P, PIECE, PACK], BF16, name="grouped%d" % i, tag=tag, align_bytes=64)
             nc.scalar.copy(
                 grouped[:].rearrange("p (c i) t -> p c t i", i=4),
                 h_raw[i][:].rearrange("p t (c i) -> p c t i", i=4),
             )
-            codes = keep.tile([P, w], U32, name="h_code%d" % i, align_bytes=64)
-            scales = keep.tile([P, w], U8, name="h_scale%d" % i, align_bytes=64)
+            return grouped
+
+        h_code, h_scale = [], []
+
+        def quantise(i, grouped, tag):
+            codes = keep.tile([P, PIECE], U32, name="h_code%d" % i, tag=tag, align_bytes=64)
+            scales = keep.tile([P, PIECE], U8, name="h_scale%d" % i, align_bytes=64)
             nc.vector.quantize_mx(
                 out=codes[:].bitcast(FP8X4), scales=scales[:], in_=grouped[:].rearrange("p w j -> p (w j)")
             )
-            for c in range(0, w, P):
+            for c in range(0, PIECE, P):
                 h_code.append(codes[:, c : c + P])
                 h_scale.append(scales[:, c : c + P])
 
-        quantise(0)
-        bias_picked = keep.tile([P, S], F32, name="bias_picked")
+        quantise(0, interleave(0, "grouped_then_bias"), "h_code0")
+        bias_picked = keep.tile([P, S], F32, name="bias_picked", tag="grouped_then_bias", align_bytes=64)
         nc.vector.tensor_copy(bias_picked[:], bias_table[:].indirect(offs_sb[:]))
-        quantise(1)
-        quantise(2)
+        grouped_second = interleave(1, "grouped1")
 
         last_code = keep.tile([P, U], F32, name="last_code")
         nc.scalar.mul(last_code[:], code_sb[:, D - 1, :], -1.0 / D)
@@ -118,10 +109,14 @@ def tile_picked_yecoc_sum_p_kernel(
         def summed_hinges(b, y, terms, offset):
             sums = [psum.tile([P, P], F32, name="sum%d" % h, tag="sum%d" % h, bufs=2) for h in range(HALVES)]
             for d in range(terms):
-                margin = keep.tile([P, U], F32, name="margin%d_%d" % (b, d))
+                first = b == 0 and d == 0
+                tag = "margin_then_codes" if first else "margin%d_%d" % (b, d)
+                margin = keep.tile([P, U], F32, name="margin", tag=tag, align_bytes=64)
                 nc.vector.tensor_tensor(margin[:], y[:].indirect(pos_sb[d][:]), code_sb[:, d, :], ALU.mult)
                 hinge = keep.tile([P, U], F32, name="hinge%d_%d" % (b, d))
                 nc.scalar.activation(hinge[:], margin[:], ACT.Relu, bias=1.0 / D, scale=-1.0 / D)
+                if first:
+                    quantise(1, grouped_second, tag)
                 for h in range(HALVES):
                     nc.tensor.matmul(
                         sums[h][:],

@@ -42,18 +42,19 @@ def tile_picked_yecoc_sum_p_kernel(
         h_rows = hT.rearrange("(p j) w -> p j w", j=PACK)
 
         nc.vector.memset(scale_table[:].bitcast(I32), 0)
-        nc.sync.dma_start(offs_sb[:], offs)
         nc.sync.dma_start(word_table[:].bitcast(I32), x_words[0].rearrange("p n t -> p (n t)").bitcast(I32))
+        nc.sync.dma_start(offs_sb[:], offs)
         for q in range(4):
             nc.sync.dma_start(
                 scale_table[32 * q : 32 * q + 4, :].bitcast(I32), x_scales[0, 4 * q : 4 * q + 4, :].bitcast(I32)
             )
         nc.sync.dma_start(h_raw[0][:], h_rows[:, :, 0:PIECE])
         nc.sync.dma_start(bias_table[:], bias)
+        nc.sync.dma_start(pos_sb[0][:], pos1)
         nc.sync.dma_start(h_raw[1][:], h_rows[:, :, PIECE:V])
-        for lst, pos in zip(pos_sb, (pos1, pos2, pos3, pos4)):
-            nc.sync.dma_start(lst[:], pos)
         nc.sync.dma_start(code_sb[:], code.rearrange("d p r -> p d r"))
+        for lst, pos in zip(pos_sb[1:], (pos2, pos3, pos4)):
+            nc.sync.dma_start(lst[:], pos)
 
         ident = keep.tile([P, P], F32, name="ident")
         make_identity(nc, ident[:])
@@ -71,87 +72,111 @@ def tile_picked_yecoc_sum_p_kernel(
             )
             return grouped
 
-        h_code, h_scale = [], []
-
-        def quantise(i, grouped, tag):
-            codes = keep.tile([P, PIECE], U32, name="h_code%d" % i, tag=tag, align_bytes=64)
+        def quantise(i, grouped):
+            codes = keep.tile([P, PIECE], U32, name="h_code%d" % i, align_bytes=64)
             scales = keep.tile([P, PIECE], U8, name="h_scale%d" % i, align_bytes=64)
             nc.vector.quantize_mx(
                 out=codes[:].bitcast(FP8X4), scales=scales[:], in_=grouped[:].rearrange("p w j -> p (w j)")
             )
-            for c in range(0, PIECE, P):
-                h_code.append(codes[:, c : c + P])
-                h_scale.append(scales[:, c : c + P])
+            return codes, scales
 
-        quantise(0, interleave(0, "grouped_then_bias"), "h_code0")
+        def product(acc, still_codes, still_scales, moving_codes, moving_scales):
+            nc.tensor.matmul_mx(
+                out=acc,
+                lhsT=still_codes.bitcast(FP8X4),
+                lhsT_scale=still_scales,
+                rhs=moving_codes.bitcast(FP8X4),
+                rhs_scale=moving_scales,
+                start=True,
+                stop=True,
+            )
+
+        h_code, h_scale = quantise(0, interleave(0, "grouped_then_bias"))
         bias_picked = keep.tile([P, S], F32, name="bias_picked", tag="grouped_then_bias", align_bytes=64)
         nc.vector.tensor_copy(bias_picked[:], bias_table[:].indirect(offs_sb[:]))
-        grouped_second = interleave(1, "grouped1")
+
+        y = [keep.tile([P, S], F32, name="y%d" % b) for b in range(BLOCKS)]
+        acc = psum.tile([P, S], F32, name="acc", tag="acc", bufs=2)
+        product(acc[:], h_code[:, 0:P], h_scale[:, 0:P], x_code[:], x_scale[:])
+        nc.vector.tensor_tensor(y[0][:], acc[:], bias_picked[:], ALU.add)
+
+        bias_turned = psum.tile([P, S // P, P], F32, name="bias_turned", tag="turn", bufs=2)
+        for c in range(S // P):
+            nc.tensor.transpose(bias_turned[:, c, :], bias_picked[:, c * P : (c + 1) * P], ident[:])
+        bias_column = keep.tile([P, S // P], F32, name="bias_column")
+        nc.scalar.copy(bias_column[:], bias_turned[:, :, 0])
+
+        def turned_scores(first, codes, scales):
+            width = codes.shape[1]
+            per_bank = S // width
+            y_turned = keep.tile([P, S // P, width], F32, name="y_turned%d" % first)
+            for c0 in range(0, S // P, per_bank):
+                acc = psum.tile([P, per_bank, width], F32, name="acc", tag="acc", bufs=2)
+                for i in range(per_bank):
+                    cols = slice((c0 + i) * P, (c0 + i + 1) * P)
+                    product(acc[:, i, :], x_code[:, cols], x_scale[:, cols], codes, scales)
+                for i in range(per_bank):
+                    c = c0 + i
+                    nc.scalar.activation(
+                        y_turned[:, c, :], acc[:, i, :], ACT.Identity, bias=bias_column[:, c : c + 1]
+                    )
+            for i in range(width // P):
+                upright = psum.tile([P, S], F32, name="upright", tag="turn", bufs=2)
+                for c in range(S // P):
+                    nc.tensor.transpose(
+                        upright[:, c * P : (c + 1) * P], y_turned[:, c, i * P : (i + 1) * P], ident[:]
+                    )
+                nc.scalar.copy(y[first + i][:], upright[:])
+
+        turned_scores(1, h_code[:, P:PIECE], h_scale[:, P:PIECE])
+        h_code, h_scale = quantise(1, interleave(1, "grouped1"))
+        turned_scores(2, h_code[:], h_scale[:])
 
         last_code = keep.tile([P, U], F32, name="last_code")
         nc.scalar.mul(last_code[:], code_sb[:, D - 1, :], -1.0 / D)
 
-        def scores(b):
-            acc = psum.tile([P, S], F32, name="acc", tag="acc", bufs=2)
-            nc.tensor.matmul_mx(
-                out=acc[:],
-                lhsT=h_code[b].bitcast(FP8X4),
-                lhsT_scale=h_scale[b],
-                rhs=x_code[:].bitcast(FP8X4),
-                rhs_scale=x_scale[:],
-                start=True,
-                stop=True,
-            )
-            y = keep.tile([P, S], F32, name="y%d" % b)
-            nc.vector.tensor_tensor(y[:], acc[:], bias_picked[:], ALU.add)
-            return y
-
-        def summed_hinges(b, y, terms, offset):
-            sums = [psum.tile([P, P], F32, name="sum%d" % h, tag="sum%d" % h, bufs=2) for h in range(HALVES)]
-            for d in range(terms):
-                first = b == 0 and d == 0
-                tag = "margin_then_codes" if first else "margin%d_%d" % (b, d)
-                margin = keep.tile([P, U], F32, name="margin", tag=tag, align_bytes=64)
-                nc.vector.tensor_tensor(margin[:], y[:].indirect(pos_sb[d][:]), code_sb[:, d, :], ALU.mult)
-                hinge = keep.tile([P, U], F32, name="hinge%d_%d" % (b, d))
-                nc.scalar.activation(hinge[:], margin[:], ACT.Relu, bias=1.0 / D, scale=-1.0 / D)
-                if first:
-                    quantise(1, grouped_second, tag)
-                for h in range(HALVES):
-                    nc.tensor.matmul(
-                        sums[h][:],
-                        hinge[:, h * P : (h + 1) * P],
-                        ident[:],
-                        start=(d == 0),
-                        stop=(d == terms - 1),
-                        is_transpose=True,
+        def summed_hinges(b, terms, offset):
+            sums = psum.tile([P, HALVES, P], F32, name="sums", tag="sums", bufs=2)
+            for d0 in range(0, terms, 1):
+                n = min(1, terms - d0)
+                margin = keep.tile([P, n, U], F32, name="margin", tag="margin%d_%d" % (b, d0))
+                for i in range(n):
+                    nc.vector.tensor_tensor(
+                        margin[:, i, :], y[b][:].indirect(pos_sb[d0 + i][:]), code_sb[:, d0 + i, :], ALU.mult
                     )
+                hinge = keep.tile([P, n, U], F32, name="hinge%d_%d" % (b, d0))
+                nc.scalar.activation(hinge[:], margin[:], ACT.Relu, bias=1.0 / D, scale=-1.0 / D)
+                for i in range(n):
+                    for h in range(HALVES):
+                        nc.tensor.matmul(
+                            sums[:, h, :],
+                            hinge[:, i, h * P : (h + 1) * P],
+                            ident[:],
+                            start=(d0 + i == 0 and h == 0),
+                            stop=(d0 + i == terms - 1 and h == HALVES - 1),
+                            is_transpose=True,
+                        )
             turned = keep.tile([P, HALVES, P], F32, name="turned%d" % b)
-            back = psum.tile([P, U], F32, name="back", tag="back", bufs=2)
+            nc.scalar.activation(turned[:], sums[:], ACT.Copy, bias=offset)
+            back = psum.tile([P, U], F32, name="back", tag="acc" if b == BLOCKS - 1 else "back", bufs=2)
             for h in range(HALVES):
-                nc.scalar.activation(turned[:, h, :], sums[h][:], ACT.Copy, bias=offset)
                 nc.tensor.transpose(back[:, h * P : (h + 1) * P], turned[:, h, :], ident[:])
             return back
 
         partial = {}
         for b in range(BLOCKS):
-            y = scores(b)
             if b < BLOCKS - LATE:
-                back = summed_hinges(b, y, D, 0.0)
+                back = summed_hinges(b, D, 0.0)
                 result = keep.tile([P, U], F32, name="result%d" % b)
                 nc.scalar.copy(result[:], back[:])
                 nc.sync.dma_start(out[b * P : (b + 1) * P, :], result[:])
             else:
-                partial[b] = (y, summed_hinges(b, y, D - 1, 1.0 / D))
+                partial[b] = summed_hinges(b, D - 1, 1.0 / D)
         last_margin = {}
         for b in range(BLOCKS - LATE, BLOCKS):
-            last_margin[b] = keep.tile([P, U], F32, name="last_margin%d" % b)
-            nc.vector.tensor_tensor(
-                last_margin[b][:], partial[b][0][:].indirect(pos_sb[D - 1][:]), last_code[:], ALU.mult
-            )
+            last_margin[b] = keep.tile([P, U], F32, name="last_margin", tag="margin%d_%d" % (BLOCKS - 1, b - 1))
+            nc.vector.tensor_tensor(last_margin[b][:], y[b][:].indirect(pos_sb[D - 1][:]), last_code[:], ALU.mult)
         for b in range(BLOCKS - LATE, BLOCKS):
             result = keep.tile([P, U], F32, name="result%d" % b)
-            nc.vector.scalar_tensor_tensor(
-                result[:], last_margin[b][:], -1.0 / D, partial[b][1][:], ALU.max, ALU.add
-            )
+            nc.vector.scalar_tensor_tensor(result[:], last_margin[b][:], -1.0 / D, partial[b][:], ALU.max, ALU.add)
             nc.sync.dma_start(out[b * P : (b + 1) * P, :], result[:])

@@ -38,7 +38,7 @@ def tile_picked_yecoc_sum_p_kernel(
         word_table = keep.tile([P, T], U32, name="word_table")
         bias_table = keep.tile([P, T], F32, name="bias_table")
         code_sb = keep.tile([P, D, U], F32, name="code_sb")
-        h_raw = [keep.tile([P, PACK, PIECE], F32, name="h_raw%d" % i) for i in range(2)]
+        h_raw = [keep.tile([P, PACK, PIECE], F32, name="h_raw", tag="h_raw%d" % i) for i in range(2)]
         h_rows = hT.rearrange("(p j) w -> p j w", j=PACK)
 
         nc.vector.memset(scale_table[:].bitcast(I32), 0)
@@ -64,17 +64,17 @@ def tile_picked_yecoc_sum_p_kernel(
         x_scale = keep.tile([P, S], U8, name="x_scale", align_bytes=64)
         nc.vector.tensor_copy(x_scale[:], scale_table[:].indirect(offs_sb[:]))
 
-        def interleave(i, tag):
-            grouped = keep.tile([P, PIECE, PACK], BF16, name="grouped%d" % i, tag=tag, align_bytes=64)
+        def interleave(rows, tag):
+            grouped = keep.tile([P, rows.shape[2], PACK], BF16, name="grouped", tag=tag, align_bytes=64)
             nc.scalar.copy(
-                grouped[:].rearrange("p (c i) t -> p c t i", i=4),
-                h_raw[i][:].rearrange("p t (c i) -> p c t i", i=4),
+                grouped[:].rearrange("p (c i) t -> p c t i", i=4), rows.rearrange("p t (c i) -> p c t i", i=4)
             )
             return grouped
 
-        def quantise(i, grouped):
-            codes = keep.tile([P, PIECE], U32, name="h_code%d" % i, align_bytes=64)
-            scales = keep.tile([P, PIECE], U8, name="h_scale%d" % i, align_bytes=64)
+        def quantise(grouped, tag, scale_tag):
+            width = grouped.shape[1]
+            codes = keep.tile([P, width], U32, name="h_code", tag=tag, align_bytes=64)
+            scales = keep.tile([P, width], U8, name="h_scale", tag=scale_tag, align_bytes=64)
             nc.vector.quantize_mx(
                 out=codes[:].bitcast(FP8X4), scales=scales[:], in_=grouped[:].rearrange("p w j -> p (w j)")
             )
@@ -91,71 +91,65 @@ def tile_picked_yecoc_sum_p_kernel(
                 stop=True,
             )
 
-        h_code, h_scale = quantise(0, interleave(0, "grouped_then_bias"))
-        bias_picked = keep.tile([P, S], F32, name="bias_picked", tag="grouped_then_bias", align_bytes=64)
+        codes0, scales0 = quantise(interleave(h_raw[0][:], "grouped0"), "codes0", "scales0")
+        bias_picked = keep.tile([P, S], F32, name="bias_picked", tag="h_raw0")
         nc.vector.tensor_copy(bias_picked[:], bias_table[:].indirect(offs_sb[:]))
 
-        y = [keep.tile([P, S], F32, name="y%d" % b) for b in range(BLOCKS)]
-        acc = psum.tile([P, S], F32, name="acc", tag="acc", bufs=2)
-        product(acc[:], h_code[:, 0:P], h_scale[:, 0:P], x_code[:], x_scale[:])
-        nc.vector.tensor_tensor(y[0][:], acc[:], bias_picked[:], ALU.add)
+        accs = []
+        for b in range(2):
+            accs.append(psum.tile([P, S], F32, name="acc", tag="acc", bufs=2))
+            cols = slice(b * P, (b + 1) * P)
+            product(accs[b][:], codes0[:, cols], scales0[:, cols], x_code[:], x_scale[:])
+        y = [keep.tile([P, S], F32, name="y0")]
+        nc.vector.tensor_tensor(y[0][:], accs[0][:], bias_picked[:], ALU.add)
+        codes2, scales2 = quantise(interleave(h_raw[1][:], "grouped2"), "hinge0_1", "hinge0_2")
+        y.append(keep.tile([P, S], F32, name="y1", tag="h_raw1"))
+        nc.vector.tensor_tensor(y[1][:], accs[1][:], bias_picked[:], ALU.add)
 
-        bias_turned = psum.tile([P, S // P, P], F32, name="bias_turned", tag="turn", bufs=2)
+        bias_turned = psum.tile([P, S // P, P], F32, name="bias_turned", tag="acc", bufs=2)
         for c in range(S // P):
             nc.tensor.transpose(bias_turned[:, c, :], bias_picked[:, c * P : (c + 1) * P], ident[:])
         bias_column = keep.tile([P, S // P], F32, name="bias_column")
         nc.scalar.copy(bias_column[:], bias_turned[:, :, 0])
 
-        def turned_scores(first, codes, scales):
-            width = codes.shape[1]
-            per_bank = S // width
-            y_turned = keep.tile([P, S // P, width], F32, name="y_turned%d" % first)
-            for c0 in range(0, S // P, per_bank):
-                acc = psum.tile([P, per_bank, width], F32, name="acc", tag="acc", bufs=2)
-                for i in range(per_bank):
-                    cols = slice((c0 + i) * P, (c0 + i + 1) * P)
-                    product(acc[:, i, :], x_code[:, cols], x_scale[:, cols], codes, scales)
-                for i in range(per_bank):
-                    c = c0 + i
-                    nc.scalar.activation(
-                        y_turned[:, c, :], acc[:, i, :], ACT.Identity, bias=bias_column[:, c : c + 1]
-                    )
-            for i in range(width // P):
-                upright = psum.tile([P, S], F32, name="upright", tag="turn", bufs=2)
-                for c in range(S // P):
-                    nc.tensor.transpose(
-                        upright[:, c * P : (c + 1) * P], y_turned[:, c, i * P : (i + 1) * P], ident[:]
-                    )
-                nc.scalar.copy(y[first + i][:], upright[:])
-
-        turned_scores(1, h_code[:, P:PIECE], h_scale[:, P:PIECE])
-        h_code, h_scale = quantise(1, interleave(1, "grouped1"))
-        turned_scores(2, h_code[:], h_scale[:])
-
         last_code = keep.tile([P, U], F32, name="last_code")
         nc.scalar.mul(last_code[:], code_sb[:, D - 1, :], -1.0 / D)
 
-        def summed_hinges(b, terms, offset):
-            sums = psum.tile([P, HALVES, P], F32, name="sums", tag="sums", bufs=2)
-            for d0 in range(0, terms, 1):
-                n = min(1, terms - d0)
-                margin = keep.tile([P, n, U], F32, name="margin", tag="margin%d_%d" % (b, d0))
-                for i in range(n):
-                    nc.vector.tensor_tensor(
-                        margin[:, i, :], y[b][:].indirect(pos_sb[d0 + i][:]), code_sb[:, d0 + i, :], ALU.mult
-                    )
-                hinge = keep.tile([P, n, U], F32, name="hinge%d_%d" % (b, d0))
-                nc.scalar.activation(hinge[:], margin[:], ACT.Relu, bias=1.0 / D, scale=-1.0 / D)
-                for i in range(n):
-                    for h in range(HALVES):
-                        nc.tensor.matmul(
-                            sums[:, h, :],
-                            hinge[:, i, h * P : (h + 1) * P],
-                            ident[:],
-                            start=(d0 + i == 0 and h == 0),
-                            stop=(d0 + i == terms - 1 and h == HALVES - 1),
-                            is_transpose=True,
-                        )
+        held = ["hinge0_3", "hinge1_0", "hinge1_1", "hinge1_2"]
+        y_turned = [keep.tile([P, PIECE], F32, name="y_turned", tag=tag, align_bytes=64) for tag in held]
+
+        def turned_scores(pair, tag):
+            acc = psum.tile([P, 2, PIECE], F32, name="acc", tag=tag, bufs=2)
+            for i in range(2):
+                cols = slice((2 * pair + i) * P, (2 * pair + i + 1) * P)
+                product(acc[:, i, :], x_code[:, cols], x_scale[:, cols], codes2[:], scales2[:])
+            for i in range(2):
+                c = 2 * pair + i
+                nc.scalar.activation(y_turned[c][:], acc[:, i, :], ACT.Identity, bias=bias_column[:, c : c + 1])
+
+        def upright_scores(i):
+            upright = psum.tile([P, S], F32, name="upright", tag="turn", bufs=2)
+            for c in range(S // P):
+                nc.tensor.transpose(upright[:, c * P : (c + 1) * P], y_turned[c][:, i * P : (i + 1) * P], ident[:])
+            y.append(keep.tile([P, S], F32, name="y%d" % (2 + i)))
+            nc.scalar.copy(y[2 + i][:], upright[:])
+
+        def add_hinge(b, d, terms, sums):
+            margin = keep.tile([P, U], F32, name="margin", tag="margin%d_%d" % (b, d))
+            nc.vector.tensor_tensor(margin[:], y[b][:].indirect(pos_sb[d][:]), code_sb[:, d, :], ALU.mult)
+            hinge = keep.tile([P, U], F32, name="hinge", tag="hinge%d_%d" % (b, d), align_bytes=64)
+            nc.scalar.activation(hinge[:], margin[:], ACT.Relu, bias=1.0 / D, scale=-1.0 / D)
+            for h in range(HALVES):
+                nc.tensor.matmul(
+                    sums[:, h, :],
+                    hinge[:, h * P : (h + 1) * P],
+                    ident[:],
+                    start=(d == 0 and h == 0),
+                    stop=(d == terms - 1 and h == HALVES - 1),
+                    is_transpose=True,
+                )
+
+        def upright_sum(b, sums, offset):
             turned = keep.tile([P, HALVES, P], F32, name="turned%d" % b)
             nc.scalar.activation(turned[:], sums[:], ACT.Copy, bias=offset)
             back = psum.tile([P, U], F32, name="back", tag="acc" if b == BLOCKS - 1 else "back", bufs=2)
@@ -163,15 +157,24 @@ def tile_picked_yecoc_sum_p_kernel(
                 nc.tensor.transpose(back[:, h * P : (h + 1) * P], turned[:, h, :], ident[:])
             return back
 
+        turned_scores(0, "turn")
+        turned_scores(1, "acc")
+        upright_scores(0)
+        upright_scores(1)
+        sums = psum.tile([P, HALVES, P], F32, name="sums", tag="sums", bufs=2)
+        for d in range(D):
+            add_hinge(0, d, D, sums)
+        back = upright_sum(0, sums, 0.0)
+        result = keep.tile([P, U], F32, name="result0")
+        nc.scalar.copy(result[:], back[:])
+        nc.sync.dma_start(out[0:P, :], result[:])
+
         partial = {}
-        for b in range(BLOCKS):
-            if b < BLOCKS - LATE:
-                back = summed_hinges(b, D, 0.0)
-                result = keep.tile([P, U], F32, name="result%d" % b)
-                nc.scalar.copy(result[:], back[:])
-                nc.sync.dma_start(out[b * P : (b + 1) * P, :], result[:])
-            else:
-                partial[b] = summed_hinges(b, D - 1, 1.0 / D)
+        for b in range(1, BLOCKS):
+            sums = psum.tile([P, HALVES, P], F32, name="sums", tag="sums", bufs=2)
+            for d in range(D - 1):
+                add_hinge(b, d, D - 1, sums)
+            partial[b] = upright_sum(b, sums, 1.0 / D)
         last_margin = {}
         for b in range(BLOCKS - LATE, BLOCKS):
             last_margin[b] = keep.tile([P, U], F32, name="last_margin", tag="margin%d_%d" % (BLOCKS - 1, b - 1))

@@ -93,7 +93,11 @@ def tile_picked_yecoc_sum_p_kernel(
 
         codes0, scales0 = quantise(interleave(h_raw[0][:], "grouped0"), "codes0", "scales0")
         bias_picked = keep.tile([P, S], F32, name="bias_picked", tag="h_raw0")
-        nc.vector.tensor_copy(bias_picked[:], bias_table[:].indirect(offs_sb[:]))
+        halves = [slice(0, S // 2), slice(S // 2, S)]
+        for h in range(2):
+            nc.vector.tensor_copy(
+                bias_picked[:, halves[h]], bias_table[:].indirect(offs_sb[:, h * S // 32 : (h + 1) * S // 32])
+            )
 
         accs = []
         for b in range(2):
@@ -101,38 +105,44 @@ def tile_picked_yecoc_sum_p_kernel(
             cols = slice(b * P, (b + 1) * P)
             product(accs[b][:], codes0[:, cols], scales0[:, cols], x_code[:], x_scale[:])
         y = [keep.tile([P, S], F32, name="y0")]
-        nc.vector.tensor_tensor(y[0][:], accs[0][:], bias_picked[:], ALU.add)
-        codes2, scales2 = quantise(interleave(h_raw[1][:], "grouped2"), "hinge0_1", "hinge0_2")
+        for h in range(2):
+            nc.vector.tensor_tensor(y[0][:, halves[h]], accs[0][:, halves[h]], bias_picked[:, halves[h]], ALU.add)
+        quantised2 = quantise(interleave(h_raw[1][:, :, 0:P], "grouped2"), "codes2", "hinge0_0")
+        grouped3 = interleave(h_raw[1][:, :, P:PIECE], "grouped3")
         y.append(keep.tile([P, S], F32, name="y1", tag="h_raw1"))
         nc.vector.tensor_tensor(y[1][:], accs[1][:], bias_picked[:], ALU.add)
+        quantised3 = quantise(grouped3, "hinge0_1", "scales3")
 
-        bias_turned = psum.tile([P, S // P, P], F32, name="bias_turned", tag="acc", bufs=2)
+        bias_turned = psum.tile([P, S // P, P], F32, name="bias_turned", tag="back", bufs=2)
         for c in range(S // P):
             nc.tensor.transpose(bias_turned[:, c, :], bias_picked[:, c * P : (c + 1) * P], ident[:])
         bias_column = keep.tile([P, S // P], F32, name="bias_column")
         nc.scalar.copy(bias_column[:], bias_turned[:, :, 0])
 
-        last_code = keep.tile([P, U], F32, name="last_code")
-        nc.scalar.mul(last_code[:], code_sb[:, D - 1, :], -1.0 / D)
+        def turned_scores(codes, scales, bank, held):
+            acc = psum.tile([P, S // P, P], F32, name="acc", tag=bank, bufs=2)
+            for c in range(S // P):
+                cols = slice(c * P, (c + 1) * P)
+                product(acc[:, c, :], x_code[:, cols], x_scale[:, cols], codes[:], scales[:])
+            y_turned = [keep.tile([P, P], F32, name="y_turned", tag=tag, align_bytes=64) for tag in held]
+            for c in range(S // P):
+                nc.scalar.activation(y_turned[c][:], acc[:, c, :], ACT.Identity, bias=bias_column[:, c : c + 1])
+            return y_turned
 
-        held = ["hinge0_3", "hinge1_0", "hinge1_1", "hinge1_2"]
-        y_turned = [keep.tile([P, PIECE], F32, name="y_turned", tag=tag, align_bytes=64) for tag in held]
-
-        def turned_scores(pair, tag):
-            acc = psum.tile([P, 2, PIECE], F32, name="acc", tag=tag, bufs=2)
-            for i in range(2):
-                cols = slice((2 * pair + i) * P, (2 * pair + i + 1) * P)
-                product(acc[:, i, :], x_code[:, cols], x_scale[:, cols], codes2[:], scales2[:])
-            for i in range(2):
-                c = 2 * pair + i
-                nc.scalar.activation(y_turned[c][:], acc[:, i, :], ACT.Identity, bias=bias_column[:, c : c + 1])
-
-        def upright_scores(i):
+        def upright_scores(y_turned):
             upright = psum.tile([P, S], F32, name="upright", tag="turn", bufs=2)
             for c in range(S // P):
-                nc.tensor.transpose(upright[:, c * P : (c + 1) * P], y_turned[c][:, i * P : (i + 1) * P], ident[:])
-            y.append(keep.tile([P, S], F32, name="y%d" % (2 + i)))
-            nc.scalar.copy(y[2 + i][:], upright[:])
+                nc.tensor.transpose(upright[:, c * P : (c + 1) * P], y_turned[c][:], ident[:])
+            y.append(keep.tile([P, S], F32, name="y%d" % len(y)))
+            nc.scalar.copy(y[-1][:], upright[:])
+
+        turned2 = turned_scores(*quantised2, "acc", ["y_turned0", "y_turned1", "y_turned2", "hinge0_2"])
+        turned3 = turned_scores(*quantised3, "acc", ["hinge0_3", "hinge1_0", "hinge1_1", "hinge1_2"])
+        upright_scores(turned2)
+        upright_scores(turned3)
+
+        last_code = keep.tile([P, U], F32, name="last_code")
+        nc.scalar.mul(last_code[:], code_sb[:, D - 1, :], -1.0 / D)
 
         def add_hinge(b, d, terms, sums):
             margin = keep.tile([P, U], F32, name="margin", tag="margin%d_%d" % (b, d))
@@ -157,10 +167,6 @@ def tile_picked_yecoc_sum_p_kernel(
                 nc.tensor.transpose(back[:, h * P : (h + 1) * P], turned[:, h, :], ident[:])
             return back
 
-        turned_scores(0, "turn")
-        turned_scores(1, "acc")
-        upright_scores(0)
-        upright_scores(1)
         sums = psum.tile([P, HALVES, P], F32, name="sums", tag="sums", bufs=2)
         for d in range(D):
             add_hinge(0, d, D, sums)

@@ -66,8 +66,10 @@ def tile_picked_yecoc_sum_p_kernel(
 
         def interleave(rows, tag):
             grouped = keep.tile([P, rows.shape[2], PACK], BF16, name="grouped", tag=tag, align_bytes=64)
-            nc.scalar.copy(
-                grouped[:].rearrange("p (c i) t -> p c t i", i=4), rows.rearrange("p t (c i) -> p c t i", i=4)
+            nc.scalar.mul(
+                grouped[:].rearrange("p (c i) t -> p c t i", i=4),
+                rows.rearrange("p t (c i) -> p c t i", i=4),
+                -1.0 / D,
             )
             return grouped
 
@@ -100,55 +102,62 @@ def tile_picked_yecoc_sum_p_kernel(
             )
 
         accs = []
-        for b in range(2):
+        for b, picked in enumerate((slice(0, S), halves[1])):
             accs.append(psum.tile([P, S], F32, name="acc", tag="acc", bufs=2))
             cols = slice(b * P, (b + 1) * P)
-            product(accs[b][:], codes0[:, cols], scales0[:, cols], x_code[:], x_scale[:])
+            product(accs[b][:, picked], codes0[:, cols], scales0[:, cols], x_code[:, picked], x_scale[:, picked])
         y = [keep.tile([P, S], F32, name="y0")]
         for h in range(2):
-            nc.vector.tensor_tensor(y[0][:, halves[h]], accs[0][:, halves[h]], bias_picked[:, halves[h]], ALU.add)
+            nc.vector.scalar_tensor_tensor(
+                y[0][:, halves[h]], bias_picked[:, halves[h]], -1.0 / D, accs[0][:, halves[h]], ALU.mult, ALU.add
+            )
         quantised2 = quantise(interleave(h_raw[1][:, :, 0:P], "grouped2"), "codes2", "hinge0_0")
         grouped3 = interleave(h_raw[1][:, :, P:PIECE], "grouped3")
         y.append(keep.tile([P, S], F32, name="y1", tag="h_raw1"))
-        nc.vector.tensor_tensor(y[1][:], accs[1][:], bias_picked[:], ALU.add)
+        nc.vector.scalar_tensor_tensor(
+            y[1][:, halves[1]], bias_picked[:, halves[1]], -1.0 / D, accs[1][:, halves[1]], ALU.mult, ALU.add
+        )
         quantised3 = quantise(grouped3, "hinge0_1", "scales3")
 
         bias_turned = psum.tile([P, S // P, P], F32, name="bias_turned", tag="back", bufs=2)
         for c in range(S // P):
             nc.tensor.transpose(bias_turned[:, c, :], bias_picked[:, c * P : (c + 1) * P], ident[:])
         bias_column = keep.tile([P, S // P], F32, name="bias_column")
-        nc.scalar.copy(bias_column[:], bias_turned[:, :, 0])
+        nc.scalar.mul(bias_column[:], bias_turned[:, :, 0], -1.0 / D)
 
         def turned_scores(codes, scales, bank, held):
-            acc = psum.tile([P, S // P, P], F32, name="acc", tag=bank, bufs=2)
-            for c in range(S // P):
+            acc = psum.tile([P, len(held), P], F32, name="acc", tag=bank, bufs=2)
+            for c in range(len(held)):
                 cols = slice(c * P, (c + 1) * P)
-                product(acc[:, c, :], x_code[:, cols], x_scale[:, cols], codes[:], scales[:])
+                product(acc[:, c, :], x_code[:, cols], x_scale[:, cols], codes, scales)
             y_turned = [keep.tile([P, P], F32, name="y_turned", tag=tag, align_bytes=64) for tag in held]
-            for c in range(S // P):
+            for c in range(len(held)):
                 nc.scalar.activation(y_turned[c][:], acc[:, c, :], ACT.Identity, bias=bias_column[:, c : c + 1])
             return y_turned
 
-        def upright_scores(y_turned):
-            upright = psum.tile([P, S], F32, name="upright", tag="turn", bufs=2)
-            for c in range(S // P):
+        def upright_scores(y_turned, scores, bank):
+            upright = psum.tile([P, len(y_turned) * P], F32, name="upright", tag=bank, bufs=2)
+            for c in range(len(y_turned)):
                 nc.tensor.transpose(upright[:, c * P : (c + 1) * P], y_turned[c][:], ident[:])
-            y.append(keep.tile([P, S], F32, name="y%d" % len(y)))
-            nc.scalar.copy(y[-1][:], upright[:])
+            nc.scalar.copy(scores, upright[:])
 
-        turned2 = turned_scores(*quantised2, "acc", ["y_turned0", "y_turned1", "y_turned2", "hinge0_2"])
-        turned3 = turned_scores(*quantised3, "acc", ["hinge0_3", "hinge1_0", "hinge1_1", "hinge1_2"])
-        upright_scores(turned2)
-        upright_scores(turned3)
-
-        last_code = keep.tile([P, U], F32, name="last_code")
-        nc.scalar.mul(last_code[:], code_sb[:, D - 1, :], -1.0 / D)
+        turned1 = turned_scores(codes0[:, P:PIECE], scales0[:, P:PIECE], "sums", ["y_turned3", "y_turned4"])
+        upright_scores(turned1, y[1][:, halves[0]], "back")
+        turned2 = turned_scores(
+            quantised2[0][:], quantised2[1][:], "acc", ["y_turned0", "y_turned1", "y_turned2", "hinge0_2"]
+        )
+        turned3 = turned_scores(
+            quantised3[0][:], quantised3[1][:], "acc", ["hinge0_3", "hinge1_0", "hinge1_1", "hinge1_2"]
+        )
+        for b, y_turned in ((2, turned2), (3, turned3)):
+            y.append(keep.tile([P, S], F32, name="y%d" % b))
+            upright_scores(y_turned, y[b][:], "turn")
 
         def add_hinge(b, d, terms, sums):
             margin = keep.tile([P, U], F32, name="margin", tag="margin%d_%d" % (b, d))
             nc.vector.tensor_tensor(margin[:], y[b][:].indirect(pos_sb[d][:]), code_sb[:, d, :], ALU.mult)
             hinge = keep.tile([P, U], F32, name="hinge", tag="hinge%d_%d" % (b, d), align_bytes=64)
-            nc.scalar.activation(hinge[:], margin[:], ACT.Relu, bias=1.0 / D, scale=-1.0 / D)
+            nc.scalar.activation(hinge[:], margin[:], ACT.Relu, bias=1.0 / D)
             for h in range(HALVES):
                 nc.tensor.matmul(
                     sums[:, h, :],
@@ -184,7 +193,7 @@ def tile_picked_yecoc_sum_p_kernel(
         last_margin = {}
         for b in range(BLOCKS - LATE, BLOCKS):
             last_margin[b] = keep.tile([P, U], F32, name="last_margin", tag="margin%d_%d" % (BLOCKS - 1, b - 1))
-            nc.vector.tensor_tensor(last_margin[b][:], y[b][:].indirect(pos_sb[D - 1][:]), last_code[:], ALU.mult)
+            nc.vector.tensor_tensor(last_margin[b][:], y[b][:].indirect(pos_sb[D - 1][:]), code_sb[:, D - 1, :], ALU.mult)
         for b in range(BLOCKS - LATE, BLOCKS):
             result = keep.tile([P, U], F32, name="result%d" % b)
             nc.vector.scalar_tensor_tensor(result[:], last_margin[b][:], -1.0 / D, partial[b][:], ALU.max, ALU.add)

@@ -102,10 +102,11 @@ def tile_picked_yecoc_sum_p_kernel(
             )
 
         accs = []
-        for b, picked in enumerate((slice(0, S), halves[1])):
+        for b, parts in enumerate(([slice(0, S)], [slice(P, S // 2), halves[1]])):
             accs.append(psum.tile([P, S], F32, name="acc", tag="acc", bufs=2))
             cols = slice(b * P, (b + 1) * P)
-            product(accs[b][:, picked], codes0[:, cols], scales0[:, cols], x_code[:, picked], x_scale[:, picked])
+            for part in parts:
+                product(accs[b][:, part], codes0[:, cols], scales0[:, cols], x_code[:, part], x_scale[:, part])
         y = [keep.tile([P, S], F32, name="y0")]
         for h in range(2):
             nc.vector.scalar_tensor_tensor(
@@ -115,7 +116,7 @@ def tile_picked_yecoc_sum_p_kernel(
         grouped3 = interleave(h_raw[1][:, :, P:PIECE], "grouped3")
         y.append(keep.tile([P, S], F32, name="y1", tag="h_raw1"))
         nc.vector.scalar_tensor_tensor(
-            y[1][:, halves[1]], bias_picked[:, halves[1]], -1.0 / D, accs[1][:, halves[1]], ALU.mult, ALU.add
+            y[1][:, P:S], bias_picked[:, P:S], -1.0 / D, accs[1][:, P:S], ALU.mult, ALU.add
         )
         quantised3 = quantise(grouped3, "hinge0_1", "scales3")
 
@@ -141,8 +142,8 @@ def tile_picked_yecoc_sum_p_kernel(
                 nc.tensor.transpose(upright[:, c * P : (c + 1) * P], y_turned[c][:], ident[:])
             nc.scalar.copy(scores, upright[:])
 
-        turned1 = turned_scores(codes0[:, P:PIECE], scales0[:, P:PIECE], "sums", ["y_turned3", "y_turned4"])
-        upright_scores(turned1, y[1][:, halves[0]], "back")
+        turned1 = turned_scores(codes0[:, P:PIECE], scales0[:, P:PIECE], "sums", ["y_turned3"])
+        upright_scores(turned1, y[1][:, 0:P], "back")
         turned2 = turned_scores(
             quantised2[0][:], quantised2[1][:], "acc", ["y_turned0", "y_turned1", "y_turned2", "hinge0_2"]
         )

@@ -20,8 +20,8 @@ P = 128
 PACK = 4
 BLOCKS = V // P
 HALVES = U // P
-LATE = 3
 PIECE = V // 2
+HALF = S // 2
 
 
 def tile_picked_yecoc_sum_p_kernel(
@@ -35,50 +35,97 @@ def tile_picked_yecoc_sum_p_kernel(
         offs_sb = keep.tile([P, S // 16], U16, name="offs_sb")
         pos_sb = [keep.tile([P, U // 16], U16, name="pos_sb%d" % d) for d in range(D)]
         scale_table = keep.tile([P, T], U8, name="scale_table")
-        word_table = keep.tile([P, T], U32, name="word_table")
+        word_table = keep.tile([P, T], U32, name="word_table", tag="word_table", align_bytes=64)
         bias_table = keep.tile([P, T], F32, name="bias_table")
-        code_sb = keep.tile([P, D, U], F32, name="code_sb")
-        h_raw = [keep.tile([P, PACK, PIECE], F32, name="h_raw", tag="h_raw%d" % i) for i in range(2)]
+        code_first = keep.tile([P, U], F32, name="code_first")
+        code_rest = keep.tile([P, D - 1, U], F32, name="code_rest")
+        code_sb = [code_first[:]] + [code_rest[:, d, :] for d in range(D - 1)]
+        placed = ctx.enter_context(tc.tile_pool(name="placed", bufs=1))
+        h_first = keep.tile([P, PACK, PIECE], F32, name="h_first")
+        h_last = placed.tile([P, PACK, PIECE], F32, name="h_last", offset=8192)
+        h_blocks = [h_first[:, :, 0:P], h_first[:, :, P:PIECE], h_last[:, :, 0:P], h_last[:, :, P:PIECE]]
         h_rows = hT.rearrange("(p j) w -> p j w", j=PACK)
 
         nc.vector.memset(scale_table[:].bitcast(I32), 0)
-        nc.sync.dma_start(word_table[:].bitcast(I32), x_words[0].rearrange("p n t -> p (n t)").bitcast(I32))
+        factor_tile = placed.tile([P, 80], F32, name="factor_tile", offset=0, align_bytes=64)
+        factor = factor_tile[:, 0:1]
+        nc.vector.memset(factor, -1.0 / D)
+        third_factor = keep.tile([P, 1], F32, name="third_factor", tag="third_factor")
+        nc.vector.memset(third_factor[:], -1.0 / D)
+        nc.vector.memset(bias_table[0 : P - 1, :], 0.0)
         nc.sync.dma_start(offs_sb[:], offs)
+        nc.sync.dma_start(bias_table[P - 1 : P, :], bias[0:1, :])
+        nc.sync.dma_start(h_first[:], h_rows[:, :, 0:PIECE])
         for q in range(4):
             nc.sync.dma_start(
                 scale_table[32 * q : 32 * q + 4, :].bitcast(I32), x_scales[0, 4 * q : 4 * q + 4, :].bitcast(I32)
             )
-        nc.sync.dma_start(h_raw[0][:], h_rows[:, :, 0:PIECE])
-        nc.sync.dma_start(bias_table[:], bias)
+        nc.sync.dma_start(word_table[:].bitcast(I32), x_words[0].rearrange("p n t -> p (n t)").bitcast(I32))
+        nc.sync.dma_start(h_last[:], h_rows[:, :, PIECE:V])
         nc.sync.dma_start(pos_sb[0][:], pos1)
-        nc.sync.dma_start(h_raw[1][:], h_rows[:, :, PIECE:V])
-        nc.sync.dma_start(code_sb[:], code.rearrange("d p r -> p d r"))
+        nc.sync.dma_start(code_first[:], code[0])
         for lst, pos in zip(pos_sb[1:], (pos2, pos3, pos4)):
             nc.sync.dma_start(lst[:], pos)
+        nc.sync.dma_start(code_rest[:], code[1:D].rearrange("d p r -> p d r"))
 
         ident = keep.tile([P, P], F32, name="ident")
         make_identity(nc, ident[:])
 
-        x_code = keep.tile([P, S], U32, name="x_code", align_bytes=64)
-        nc.vector.tensor_copy(x_code[:], word_table[:].indirect(offs_sb[:]))
-        x_scale = keep.tile([P, S], U8, name="x_scale", align_bytes=64)
-        nc.vector.tensor_copy(x_scale[:], scale_table[:].indirect(offs_sb[:]))
+        halves = [slice(0, HALF), slice(HALF, S)]
+        offs_halves = [offs_sb[:, 0 : S // 32], offs_sb[:, S // 32 : S // 16]]
 
-        def interleave(rows, tag):
-            grouped = keep.tile([P, rows.shape[2], PACK], BF16, name="grouped", tag=tag, align_bytes=64)
-            nc.scalar.mul(
-                grouped[:].rearrange("p (c i) t -> p c t i", i=4),
+        def bank(n, shape):
+            return psum.tile(shape, F32, name="bank", tag="bank%d" % n)
+
+        turned_bias = []
+        for h in range(2):
+            picked = keep.tile([P, HALF], F32, name="picked", tag="picked%d" % h, align_bytes=64)
+            nc.vector.tensor_copy(picked[:], bias_table[:].indirect(offs_halves[h]))
+            turned_bias.append(bank(h, [P, 2, P]))
+            for c in range(2):
+                nc.tensor.transpose(turned_bias[h][:, c, :], picked[:, c * P : (c + 1) * P], ident[:])
+
+        def interleave(b, grouped):
+            rows = h_blocks[b]
+            nc.scalar.activation(
+                grouped.rearrange("p (c i) t -> p c t i", i=4),
                 rows.rearrange("p t (c i) -> p c t i", i=4),
-                -1.0 / D,
+                ACT.Copy,
+                scale=third_factor[:] if b == 2 else -1.0 / D,
             )
             return grouped
 
-        def quantise(grouped, tag, scale_tag):
-            width = grouped.shape[1]
-            codes = keep.tile([P, width], U32, name="h_code", tag=tag, align_bytes=64)
-            scales = keep.tile([P, width], U8, name="h_scale", tag=scale_tag, align_bytes=64)
+        def bias_to_columns(h, columns):
+            nc.scalar.activation(columns, turned_bias[h][:, :, P - 1], ACT.Copy, scale=factor)
+
+        def spread_bias(h, columns):
+            spread = bank(2 + h, [P, HALF])
+            for c in range(2):
+                nc.tensor.transpose(
+                    spread[:, c * P : (c + 1) * P], columns[:, c : c + 1].to_broadcast([P, P]), ident[:]
+                )
+            return spread
+
+        grouped_first = keep.tile([P, P, PACK], BF16, name="grouped_first", tag="grouped_first", align_bytes=64)
+        interleave(0, grouped_first[:])
+        bias_column = [keep.tile([P, 2], F32, name="bias_column%d" % h) for h in range(2)]
+        bias_to_columns(0, bias_column[0][:])
+        grouped_second = keep.tile([P, P, PACK], BF16, name="grouped_second", align_bytes=64)
+        interleave(1, grouped_second[:])
+        bias_to_columns(1, bias_column[1][:])
+        spread_banks = [spread_bias(h, bias_column[h][:]) for h in range(2)]
+        bias_spread = keep.tile([P, S], F32, name="bias_spread")
+        for h in range(2):
+            nc.scalar.copy(bias_spread[:, halves[h]], spread_banks[h][:])
+
+        def quantise(b, grouped):
+            codes = keep.tile([P, P], U32, name="h_code%d" % b, align_bytes=64)
+            if b < 2:
+                scales = placed.tile([P, P], U8, name="h_scale%d" % b, offset=b * P, align_bytes=64)
+            else:
+                scales = keep.tile([P, P], U8, name="h_scale%d" % b, align_bytes=64)
             nc.vector.quantize_mx(
-                out=codes[:].bitcast(FP8X4), scales=scales[:], in_=grouped[:].rearrange("p w j -> p (w j)")
+                out=codes[:].bitcast(FP8X4), scales=scales[:], in_=grouped.rearrange("p w j -> p (w j)")
             )
             return codes, scales
 
@@ -93,109 +140,128 @@ def tile_picked_yecoc_sum_p_kernel(
                 stop=True,
             )
 
-        codes0, scales0 = quantise(interleave(h_raw[0][:], "grouped0"), "codes0", "scales0")
-        bias_picked = keep.tile([P, S], F32, name="bias_picked", tag="h_raw0")
-        halves = [slice(0, S // 2), slice(S // 2, S)]
-        for h in range(2):
-            nc.vector.tensor_copy(
-                bias_picked[:, halves[h]], bias_table[:].indirect(offs_sb[:, h * S // 32 : (h + 1) * S // 32])
-            )
+        x_scale = keep.tile([P, S], U8, name="x_scale", align_bytes=64)
+        nc.vector.tensor_copy(x_scale[:], scale_table[:].indirect(offs_sb[:]))
+        x_code = [
+            keep.tile([P, HALF], U32, name="x_code0", align_bytes=64),
+            placed.tile([P, HALF], U32, name="x_code1", offset=2 * P, align_bytes=64),
+        ]
+        nc.vector.tensor_copy(x_code[0][:], word_table[:].indirect(offs_halves[0]))
+        quantised = [quantise(0, grouped_first[:])]
+        for c in range(2):
+            quarter = offs_sb[:, (2 + c) * P // 16 : (3 + c) * P // 16]
+            nc.vector.tensor_copy(x_code[1][:, c * P : (c + 1) * P], word_table[:].indirect(quarter))
+        quantised.append(quantise(1, grouped_second[:]))
 
-        accs = []
-        for b, parts in enumerate(([slice(0, S)], [slice(P, S // 2), halves[1]])):
-            accs.append(psum.tile([P, S], F32, name="acc", tag="acc", bufs=2))
-            cols = slice(b * P, (b + 1) * P)
-            for part in parts:
-                product(accs[b][:, part], codes0[:, cols], scales0[:, cols], x_code[:, part], x_scale[:, part])
-        y = [keep.tile([P, S], F32, name="y0")]
-        for h in range(2):
-            nc.vector.scalar_tensor_tensor(
-                y[0][:, halves[h]], bias_picked[:, halves[h]], -1.0 / D, accs[0][:, halves[h]], ALU.mult, ALU.add
-            )
-        quantised2 = quantise(interleave(h_raw[1][:, :, 0:P], "grouped2"), "codes2", "hinge0_0")
-        grouped3 = interleave(h_raw[1][:, :, P:PIECE], "grouped3")
-        y.append(keep.tile([P, S], F32, name="y1", tag="h_raw1"))
-        nc.vector.scalar_tensor_tensor(
-            y[1][:, P:S], bias_picked[:, P:S], -1.0 / D, accs[1][:, P:S], ALU.mult, ALU.add
+        y = {b: keep.tile([P, S], F32, name="y%d" % b) for b in (0, 2, 3)}
+        pieces = (
+            (0, x_code[0][:], slice(0, HALF)),
+            (1, x_code[1][:, 0:P], slice(HALF, HALF + P)),
+            (4, x_code[1][:, P:HALF], slice(HALF + P, S)),
         )
-        quantised3 = quantise(grouped3, "hinge0_1", "scales3")
+        for n, codes, cols in pieces:
+            acc = bank(n, [P, codes.shape[1]])
+            product(acc[:], quantised[0][0][:], quantised[0][1][:], codes, x_scale[:, cols])
+            nc.vector.tensor_tensor(y[0][:, cols], acc[:], bias_spread[:, cols], ALU.add)
+        margins = {}
 
-        bias_turned = psum.tile([P, S // P, P], F32, name="bias_turned", tag="back", bufs=2)
-        for c in range(S // P):
-            nc.tensor.transpose(bias_turned[:, c, :], bias_picked[:, c * P : (c + 1) * P], ident[:])
-        bias_column = keep.tile([P, S // P], F32, name="bias_column")
-        nc.scalar.mul(bias_column[:], bias_turned[:, :, 0], -1.0 / D)
+        def gather_margin(b, d):
+            if b == 0:
+                margins[b, d] = (first_pair if d < 2 else second_pair)[:, d % 2, :]
+            else:
+                tag = {(1, 0): "third_factor", (3, 3): "last_hinge"}.get((b, d), "margin%d_%d" % (b, d))
+                margin = keep.tile([P, U], F32, name="margin", tag=tag)
+                margins[b, d] = margin[:]
+            nc.vector.tensor_tensor(margins[b, d], y[b][:].indirect(pos_sb[d][:]), code_sb[d], ALU.mult)
 
-        def turned_scores(codes, scales, bank, held):
-            acc = psum.tile([P, len(held), P], F32, name="acc", tag=bank, bufs=2)
-            for c in range(len(held)):
+        grouped_last = keep.tile([P, PIECE, PACK], BF16, name="grouped_last", tag="word_table", align_bytes=64)
+        for b in (2, 3):
+            quantised.append(quantise(b, interleave(b, grouped_last[:, (b - 2) * P : (b - 1) * P, :])))
+            if b == 2:
+                first_pair = keep.tile([P, 2, U], F32, name="first_pair", tag="third_factor")
+                gather_margin(0, 0)
+                gather_margin(0, 1)
+        acc = bank(0, [P, S])
+        y[1] = placed.tile([P, S], F32, name="y1", offset=8192)
+        second_pair = placed.tile([P, 2, U], F32, name="second_pair", offset=8192 + 2048)
+        for h in range(2):
+            product(acc[:, halves[h]], quantised[1][0][:], quantised[1][1][:], x_code[h][:], x_scale[:, halves[h]])
+        nc.vector.tensor_tensor(y[1][:], acc[:], bias_spread[:], ALU.add)
+
+        turned = {}
+        TURNED_AT = {2: 16384, 3: 16384 + 4096}
+        for b, n in ((2, 5), (3, 6)):
+            acc = bank(n, [P, S // P, P])
+            for c in range(S // P):
                 cols = slice(c * P, (c + 1) * P)
-                product(acc[:, c, :], x_code[:, cols], x_scale[:, cols], codes, scales)
-            y_turned = [keep.tile([P, P], F32, name="y_turned", tag=tag, align_bytes=64) for tag in held]
-            for c in range(len(held)):
-                nc.scalar.activation(y_turned[c][:], acc[:, c, :], ACT.Identity, bias=bias_column[:, c : c + 1])
-            return y_turned
+                codes = x_code[c // 2][:, (c % 2) * P : (c % 2 + 1) * P]
+                product(acc[:, c, :], codes, x_scale[:, cols], quantised[b][0][:], quantised[b][1][:])
+            turned[b] = placed.tile([P, S // P, P], F32, name="y_turned%d" % b, offset=TURNED_AT[b])
+            for c in range(S // P):
+                column = bias_column[c // 2][:, c % 2 : c % 2 + 1]
+                nc.scalar.activation(turned[b][:, c, :], acc[:, c, :], ACT.Identity, bias=column)
+        for b in (2, 3):
+            upright = bank(b, [P, S])
+            for c in range(S // P):
+                nc.tensor.transpose(upright[:, c * P : (c + 1) * P], turned[b][:, c, :], ident[:])
+            nc.scalar.copy(y[b][:], upright[:])
 
-        def upright_scores(y_turned, scores, bank):
-            upright = psum.tile([P, len(y_turned) * P], F32, name="upright", tag=bank, bufs=2)
-            for c in range(len(y_turned)):
-                nc.tensor.transpose(upright[:, c * P : (c + 1) * P], y_turned[c][:], ident[:])
-            nc.scalar.copy(scores, upright[:])
+        held = [(0, 1), (0, 2), (0, 3), (1, 1), (1, 2), (1, 3)]
 
-        turned1 = turned_scores(codes0[:, P:PIECE], scales0[:, P:PIECE], "sums", ["y_turned3"])
-        upright_scores(turned1, y[1][:, 0:P], "back")
-        turned2 = turned_scores(
-            quantised2[0][:], quantised2[1][:], "acc", ["y_turned0", "y_turned1", "y_turned2", "hinge0_2"]
-        )
-        turned3 = turned_scores(
-            quantised3[0][:], quantised3[1][:], "acc", ["hinge0_3", "hinge1_0", "hinge1_1", "hinge1_2"]
-        )
-        for b, y_turned in ((2, turned2), (3, turned3)):
-            y.append(keep.tile([P, S], F32, name="y%d" % b))
-            upright_scores(y_turned, y[b][:], "turn")
-
-        def add_hinge(b, d, terms, sums):
-            margin = keep.tile([P, U], F32, name="margin", tag="margin%d_%d" % (b, d))
-            nc.vector.tensor_tensor(margin[:], y[b][:].indirect(pos_sb[d][:]), code_sb[:, d, :], ALU.mult)
-            hinge = keep.tile([P, U], F32, name="hinge", tag="hinge%d_%d" % (b, d), align_bytes=64)
-            nc.scalar.activation(hinge[:], margin[:], ACT.Relu, bias=1.0 / D)
+        def add_hinge(b, d, first, last, sums):
+            if (b, d) not in margins:
+                gather_margin(b, d)
+            if (b, d) in held:
+                n = held.index((b, d))
+                at = TURNED_AT[2 + n // 3] + 32 + (n % 3 - 1) * 1024
+                hinge = placed.tile([P, U], F32, name="hinge%d_%d" % (b, d), offset=at)
+            else:
+                hinge = keep.tile([P, U], F32, name="hinge%d_%d" % (b, d))
+            nc.scalar.activation(hinge[:], margins[b, d], ACT.Relu, bias=1.0 / D)
             for h in range(HALVES):
                 nc.tensor.matmul(
                     sums[:, h, :],
                     hinge[:, h * P : (h + 1) * P],
                     ident[:],
-                    start=(d == 0 and h == 0),
-                    stop=(d == terms - 1 and h == HALVES - 1),
+                    start=(d == first and h == 0),
+                    stop=(d == last and h == HALVES - 1),
                     is_transpose=True,
                 )
 
-        def upright_sum(b, sums, offset):
-            turned = keep.tile([P, HALVES, P], F32, name="turned%d" % b)
-            nc.scalar.activation(turned[:], sums[:], ACT.Copy, bias=offset)
-            back = psum.tile([P, U], F32, name="back", tag="acc" if b == BLOCKS - 1 else "back", bufs=2)
+        for b, terms, n_sums, n_back in ((0, (0, 1, 2, 3), 4, 1), (1, (1, 2, 3, 0), 7, 0), (2, (0, 1, 2, 3), 5, 6)):
+            sums = bank(n_sums, [P, HALVES, P])
+            for d in terms:
+                add_hinge(b, d, terms[0], terms[-1], sums)
+            summed = keep.tile([P, HALVES, P], F32, name="summed%d" % b)
+            nc.scalar.copy(summed[:], sums[:])
+            back = bank(n_back, [P, U])
             for h in range(HALVES):
-                nc.tensor.transpose(back[:, h * P : (h + 1) * P], turned[:, h, :], ident[:])
-            return back
-
-        sums = psum.tile([P, HALVES, P], F32, name="sums", tag="sums", bufs=2)
-        for d in range(D):
-            add_hinge(0, d, D, sums)
-        back = upright_sum(0, sums, 0.0)
-        result = keep.tile([P, U], F32, name="result0")
-        nc.scalar.copy(result[:], back[:])
-        nc.sync.dma_start(out[0:P, :], result[:])
-
-        partial = {}
-        for b in range(1, BLOCKS):
-            sums = psum.tile([P, HALVES, P], F32, name="sums", tag="sums", bufs=2)
-            for d in range(D - 1):
-                add_hinge(b, d, D - 1, sums)
-            partial[b] = upright_sum(b, sums, 1.0 / D)
-        last_margin = {}
-        for b in range(BLOCKS - LATE, BLOCKS):
-            last_margin[b] = keep.tile([P, U], F32, name="last_margin", tag="margin%d_%d" % (BLOCKS - 1, b - 1))
-            nc.vector.tensor_tensor(last_margin[b][:], y[b][:].indirect(pos_sb[D - 1][:]), code_sb[:, D - 1, :], ALU.mult)
-        for b in range(BLOCKS - LATE, BLOCKS):
+                nc.tensor.transpose(back[:, h * P : (h + 1) * P], summed[:, h, :], ident[:])
             result = keep.tile([P, U], F32, name="result%d" % b)
-            nc.vector.scalar_tensor_tensor(result[:], last_margin[b][:], -1.0 / D, partial[b][:], ALU.max, ALU.add)
+            nc.scalar.copy(result[:], back[:])
             nc.sync.dma_start(out[b * P : (b + 1) * P, :], result[:])
+
+        last = BLOCKS - 1
+        gather_margin(last, 0)
+        hinge = keep.tile([P, U], F32, name="last_hinge", tag="last_hinge")
+        nc.scalar.activation(hinge[:], margins[last, 0], ACT.Relu, bias=1.0 / D)
+        one_term = keep.tile([P, U], F32, name="one_term")
+        nc.scalar.activation(one_term[:], hinge[:], ACT.Copy, bias=(D - 1.0) / D)
+        gather_margin(last, 1)
+        gather_margin(last, 2)
+        two_terms = keep.tile([P, U], F32, name="two_terms")
+        nc.vector.scalar_tensor_tensor(two_terms[:], margins[last, 1], -1.0 / D, one_term[:], ALU.max, ALU.add)
+        gather_margin(last, 3)
+        three_terms = [keep.tile([P, P], F32, name="three_terms%d" % h) for h in range(HALVES)]
+        for h in range(HALVES):
+            cols = slice(h * P, (h + 1) * P)
+            nc.vector.scalar_tensor_tensor(
+                three_terms[h][:], margins[last, 2][:, cols], -1.0 / D, two_terms[:, cols], ALU.max, ALU.add
+            )
+        result = keep.tile([P, U], F32, name="result%d" % last)
+        for h in range(HALVES):
+            cols = slice(h * P, (h + 1) * P)
+            nc.vector.scalar_tensor_tensor(
+                result[:, cols], margins[last, 3][:, cols], -1.0 / D, three_terms[h][:], ALU.max, ALU.add
+            )
+        nc.sync.dma_start(out[last * P : (last + 1) * P, :], result[:])

@@ -169,7 +169,7 @@ def tile_picked_yecoc_sum_p_kernel(
             if b == 0:
                 margins[b, d] = (first_pair if d < 2 else second_pair)[:, d % 2, :]
             else:
-                tag = {(1, 0): "third_factor", (3, 3): "last_hinge"}.get((b, d), "margin%d_%d" % (b, d))
+                tag = "third_factor" if (b, d) == (1, 0) else "margin%d_%d" % (b, d)
                 margin = keep.tile([P, U], F32, name="margin", tag=tag)
                 margins[b, d] = margin[:]
             nc.vector.tensor_tensor(margins[b, d], y[b][:].indirect(pos_sb[d][:]), code_sb[d], ALU.mult)
@@ -239,15 +239,14 @@ def tile_picked_yecoc_sum_p_kernel(
                 nc.tensor.transpose(back[:, h * P : (h + 1) * P], summed[:, h, :], ident[:])
             result = keep.tile([P, U], F32, name="result%d" % b)
             nc.scalar.copy(result[:], back[:])
-            nc.sync.dma_start(out[b * P : (b + 1) * P, :], result[:])
+            queue = nc.sync if b == 0 else nc.scalar
+            queue.dma_start(out[b * P : (b + 1) * P, :], result[:])
 
         last = BLOCKS - 1
-        gather_margin(last, 0)
-        hinge = keep.tile([P, U], F32, name="last_hinge", tag="last_hinge")
-        nc.scalar.activation(hinge[:], margins[last, 0], ACT.Relu, bias=1.0 / D)
+        for d in range(2):
+            gather_margin(last, d)
         one_term = keep.tile([P, U], F32, name="one_term")
-        nc.scalar.activation(one_term[:], hinge[:], ACT.Copy, bias=(D - 1.0) / D)
-        gather_margin(last, 1)
+        nc.vector.tensor_scalar(one_term[:], margins[last, 0], -1.0 / D, 1.0, ALU.max, ALU.add)
         gather_margin(last, 2)
         two_terms = keep.tile([P, U], F32, name="two_terms")
         nc.vector.scalar_tensor_tensor(two_terms[:], margins[last, 1], -1.0 / D, one_term[:], ALU.max, ALU.add)

@@ -20,8 +20,11 @@ P = 128
 PACK = 4
 BLOCKS = V // P
 HALVES = U // P
-PIECE = V // 2
 HALF = S // 2
+TURNED = 2
+CHAINED = D - TURNED
+PIECES = TURNED * HALVES
+AHEAD = 2
 
 
 def tile_picked_yecoc_sum_p_kernel(
@@ -32,41 +35,58 @@ def tile_picked_yecoc_sum_p_kernel(
         keep = ctx.enter_context(tc.tile_pool(name="keep", bufs=1))
         psum = ctx.enter_context(tc.psum_pool(name="psum", bufs=1))
 
+        placed = ctx.enter_context(tc.tile_pool(name="placed", bufs=1))
+
         offs_sb = keep.tile([P, S // 16], U16, name="offs_sb")
         pos_sb = [keep.tile([P, U // 16], U16, name="pos_sb%d" % d) for d in range(D)]
         scale_table = keep.tile([P, T], U8, name="scale_table")
-        word_table = keep.tile([P, T], U32, name="word_table", tag="word_table", align_bytes=64)
+        word_table = keep.tile([P, T], U32, name="word_table", align_bytes=64)
         bias_table = keep.tile([P, T], F32, name="bias_table")
-        code_first = keep.tile([P, U], F32, name="code_first")
-        code_rest = keep.tile([P, D - 1, U], F32, name="code_rest")
-        code_sb = [code_first[:]] + [code_rest[:, d, :] for d in range(D - 1)]
-        placed = ctx.enter_context(tc.tile_pool(name="placed", bufs=1))
-        h_first = keep.tile([P, PACK, PIECE], F32, name="h_first")
-        h_last = placed.tile([P, PACK, PIECE], F32, name="h_last", offset=8192)
-        h_blocks = [h_first[:, :, 0:P], h_first[:, :, P:PIECE], h_last[:, :, 0:P], h_last[:, :, P:PIECE]]
+        code_rows = [keep.tile([P, U], F32, name="code_rows%d" % d) for d in range(CHAINED)]
+        code_pieces = keep.tile([P, P], F32, name="code_pieces")
+        h_0 = keep.tile([P, PACK, P], F32, name="h_0")
+        h_1 = keep.tile([P, PACK, P], F32, name="h_1")
+        h_last = keep.tile([P, PACK, 2 * P], F32, name="h_last", tag="h_last")
+        h_blocks = [h_0[:], h_1[:], h_last[:, :, 0:P], h_last[:, :, P : 2 * P]]
         h_rows = hT.rearrange("(p j) w -> p j w", j=PACK)
 
-        nc.vector.memset(scale_table[:].bitcast(I32), 0)
-        factor_tile = placed.tile([P, 80], F32, name="factor_tile", offset=0, align_bytes=64)
-        factor = factor_tile[:, 0:1]
-        nc.vector.memset(factor, -1.0 / D)
-        third_factor = keep.tile([P, 1], F32, name="third_factor", tag="third_factor")
-        nc.vector.memset(third_factor[:], -1.0 / D)
+        def constant(name, value):
+            column = keep.tile([P, 1], F32, name=name, tag=name, align_bytes=64)
+            nc.vector.memset(column[:], value)
+            return column
+
+        nc.gpsimd.memset(scale_table[:].bitcast(I32), 0)
+        quarter_tile = placed.tile([P, 768], F32, name="quarter_tile", offset=12288, align_bytes=64)
+        quarter = quarter_tile[:, 0:1]
+        nc.vector.memset(quarter, 1.0 / D)
+        share = keep.tile([P, 1], F32, name="share")
+        nc.scalar.activation(share[:], quarter, ACT.Copy, scale=float(CHAINED))
+        sign_tile = placed.tile([P, 80], F32, name="sign_tile", offset=0, align_bytes=64)
+        sign = sign_tile[:, 0:1]
+        nc.vector.memset(sign, -1.0)
+        factor = constant("factor", -1.0 / D)
         nc.vector.memset(bias_table[0 : P - 1, :], 0.0)
         nc.sync.dma_start(offs_sb[:], offs)
         nc.sync.dma_start(bias_table[P - 1 : P, :], bias[0:1, :])
-        nc.sync.dma_start(h_first[:], h_rows[:, :, 0:PIECE])
         for q in range(4):
             nc.sync.dma_start(
                 scale_table[32 * q : 32 * q + 4, :].bitcast(I32), x_scales[0, 4 * q : 4 * q + 4, :].bitcast(I32)
             )
+        nc.sync.dma_start(h_0[:], h_rows[:, :, 0:P])
         nc.sync.dma_start(word_table[:].bitcast(I32), x_words[0].rearrange("p n t -> p (n t)").bitcast(I32))
-        nc.sync.dma_start(h_last[:], h_rows[:, :, PIECE:V])
+        nc.sync.dma_start(pos_sb[2][:], pos3)
+        nc.sync.dma_start(code_rows[0][:], code[TURNED])
+        nc.sync.dma_start(h_1[:], h_rows[:, :, P : 2 * P])
+        nc.sync.dma_start(h_last[:], h_rows[:, :, 2 * P : V])
         nc.sync.dma_start(pos_sb[0][:], pos1)
-        nc.sync.dma_start(code_first[:], code[0])
-        for lst, pos in zip(pos_sb[1:], (pos2, pos3, pos4)):
-            nc.sync.dma_start(lst[:], pos)
-        nc.sync.dma_start(code_rest[:], code[1:D].rearrange("d p r -> p d r"))
+        nc.sync.dma_start(pos_sb[1][:], pos2)
+        nc.sync.dma_start(pos_sb[3][:], pos4)
+        nc.sync.dma_start(code_rows[1][:], code[TURNED + 1])
+
+        nc.gpsimd.memset(code_pieces[0 : P - PIECES, :], 0.0)
+        step = (P * U + U) // 2
+        spaced = code.rearrange("d p r -> (d p r)")[0 : PIECES * step].rearrange("(j x) -> j x", x=step)
+        nc.gpsimd.dma_start(code_pieces[P - PIECES : P, :], spaced[:, 0:P])
 
         ident = keep.tile([P, P], F32, name="ident")
         make_identity(nc, ident[:])
@@ -77,190 +97,166 @@ def tile_picked_yecoc_sum_p_kernel(
         def bank(n, shape):
             return psum.tile(shape, F32, name="bank", tag="bank%d" % n)
 
+        bias_spread = []
         turned_bias = []
         for h in range(2):
-            picked = keep.tile([P, HALF], F32, name="picked", tag="picked%d" % h, align_bytes=64)
-            nc.vector.tensor_copy(picked[:], bias_table[:].indirect(offs_halves[h]))
+            picked = keep.tile([P, HALF], F32, name="picked%d" % h)
+            nc.scalar.activation(picked[:], bias_table[:].indirect(offs_halves[h]), ACT.Copy)
             turned_bias.append(bank(h, [P, 2, P]))
             for c in range(2):
                 nc.tensor.transpose(turned_bias[h][:, c, :], picked[:, c * P : (c + 1) * P], ident[:])
 
         def interleave(b, grouped):
-            rows = h_blocks[b]
             nc.scalar.activation(
                 grouped.rearrange("p (c i) t -> p c t i", i=4),
-                rows.rearrange("p t (c i) -> p c t i", i=4),
+                h_blocks[b].rearrange("p t (c i) -> p c t i", i=4),
                 ACT.Copy,
-                scale=third_factor[:] if b == 2 else -1.0 / D,
+                scale=factor[:] if b == 1 else -1.0 / D,
             )
-            return grouped
 
-        def bias_to_columns(h, columns):
-            nc.scalar.activation(columns, turned_bias[h][:, :, P - 1], ACT.Copy, scale=factor)
-
-        def spread_bias(h, columns):
+        for h in range(2):
+            columns = keep.tile([P, 2], F32, name="bias_columns%d" % h)
+            nc.scalar.activation(columns[:], turned_bias[h][:, :, P - 1], ACT.Copy, scale=sign)
             spread = bank(2 + h, [P, HALF])
             for c in range(2):
                 nc.tensor.transpose(
                     spread[:, c * P : (c + 1) * P], columns[:, c : c + 1].to_broadcast([P, P]), ident[:]
                 )
-            return spread
+            bias_spread.append(spread)
 
-        grouped_first = keep.tile([P, P, PACK], BF16, name="grouped_first", tag="grouped_first", align_bytes=64)
-        interleave(0, grouped_first[:])
-        bias_column = [keep.tile([P, 2], F32, name="bias_column%d" % h) for h in range(2)]
-        bias_to_columns(0, bias_column[0][:])
-        grouped_second = keep.tile([P, P, PACK], BF16, name="grouped_second", align_bytes=64)
-        interleave(1, grouped_second[:])
-        bias_to_columns(1, bias_column[1][:])
-        spread_banks = [spread_bias(h, bias_column[h][:]) for h in range(2)]
-        bias_spread = keep.tile([P, S], F32, name="bias_spread")
+        bias_rows = keep.tile([P, S], F32, name="bias_rows", tag="bias_rows")
         for h in range(2):
-            nc.scalar.copy(bias_spread[:, halves[h]], spread_banks[h][:])
-
-        def quantise(b, grouped):
-            codes = keep.tile([P, P], U32, name="h_code%d" % b, align_bytes=64)
-            if b < 2:
-                scales = placed.tile([P, P], U8, name="h_scale%d" % b, offset=b * P, align_bytes=64)
-            else:
-                scales = keep.tile([P, P], U8, name="h_scale%d" % b, align_bytes=64)
-            nc.vector.quantize_mx(
-                out=codes[:].bitcast(FP8X4), scales=scales[:], in_=grouped.rearrange("p w j -> p (w j)")
-            )
-            return codes, scales
-
-        def product(acc, still_codes, still_scales, moving_codes, moving_scales):
-            nc.tensor.matmul_mx(
-                out=acc,
-                lhsT=still_codes.bitcast(FP8X4),
-                lhsT_scale=still_scales,
-                rhs=moving_codes.bitcast(FP8X4),
-                rhs_scale=moving_scales,
-                start=True,
-                stop=True,
-            )
+            nc.scalar.activation(bias_rows[:, halves[h]], bias_spread[h][:], ACT.Copy, scale=quarter)
+        turned_code = bank(2, [P, P])
+        nc.tensor.transpose(turned_code[:], code_pieces[:], ident[:])
+        grouped_first = keep.tile([P, P, PACK], BF16, name="grouped_first", align_bytes=64)
+        grouped = [grouped_first[:]]
+        for b in range(1, BLOCKS):
+            at = 12288 + 1024 * (b - 1)
+            grouped.append(placed.tile([P, P, PACK], BF16, name="grouped%d" % b, offset=at, align_bytes=64)[:])
+        for b in range(1, BLOCKS):
+            interleave(b, grouped[b])
+        code_columns = keep.tile([P, PIECES], F32, name="code_columns", tag="h_last")
+        nc.scalar.copy(code_columns[:], turned_code[:, P - PIECES : P])
 
         x_scale = keep.tile([P, S], U8, name="x_scale", align_bytes=64)
         nc.vector.tensor_copy(x_scale[:], scale_table[:].indirect(offs_sb[:]))
+        nc.vector.tensor_scalar_mul(
+            grouped[0].rearrange("p (c i) t -> p c t i", i=4), h_0[:].rearrange("p t (c i) -> p c t i", i=4), -1.0 / D
+        )
         x_code = [
             keep.tile([P, HALF], U32, name="x_code0", align_bytes=64),
             placed.tile([P, HALF], U32, name="x_code1", offset=2 * P, align_bytes=64),
         ]
-        nc.vector.tensor_copy(x_code[0][:], word_table[:].indirect(offs_halves[0]))
-        quantised = [quantise(0, grouped_first[:])]
-        for c in range(2):
-            quarter = offs_sb[:, (2 + c) * P // 16 : (3 + c) * P // 16]
-            nc.vector.tensor_copy(x_code[1][:, c * P : (c + 1) * P], word_table[:].indirect(quarter))
-        quantised.append(quantise(1, grouped_second[:]))
 
-        y = {b: keep.tile([P, S], F32, name="y%d" % b) for b in (0, 2, 3)}
-        pieces = (
-            (0, x_code[0][:], slice(0, HALF)),
-            (1, x_code[1][:, 0:P], slice(HALF, HALF + P)),
-            (4, x_code[1][:, P:HALF], slice(HALF + P, S)),
-        )
-        for n, codes, cols in pieces:
-            acc = bank(n, [P, codes.shape[1]])
-            product(acc[:], quantised[0][0][:], quantised[0][1][:], codes, x_scale[:, cols])
-            nc.vector.tensor_tensor(y[0][:, cols], acc[:], bias_spread[:, cols], ALU.add)
+        y = [keep.tile([P, S], F32, name="y%d" % b) for b in range(BLOCKS)]
+
+        def quantise(b):
+            codes = keep.tile([P, P], U32, name="h_code%d" % b, align_bytes=64)
+            if b == 0:
+                scales = placed.tile([P, P], U8, name="h_scale0", offset=0, align_bytes=64)
+            else:
+                scales = keep.tile([P, P], U8, name="h_scale%d" % b, align_bytes=64)
+            nc.vector.quantize_mx(
+                out=codes[:].bitcast(FP8X4), scales=scales[:], in_=grouped[b].rearrange("p w j -> p (w j)")
+            )
+            return codes, scales
+
+        def product(acc, still, h):
+            nc.tensor.matmul_mx(
+                out=acc,
+                lhsT=still[0][:].bitcast(FP8X4),
+                lhsT_scale=still[1][:],
+                rhs=x_code[h][:].bitcast(FP8X4),
+                rhs_scale=x_scale[:, halves[h]],
+                start=True,
+                stop=True,
+            )
+
+        nc.vector.tensor_copy(x_code[0][:], word_table[:].indirect(offs_halves[0]))
+        still = quantise(0)
+        nc.vector.tensor_copy(x_code[1][:], word_table[:].indirect(offs_halves[1]))
+        for h in range(2):
+            acc = bank(4 + h, [P, HALF])
+            product(acc[:], still, h)
+            nc.vector.tensor_tensor(y[0][:, halves[h]], acc[:], bias_rows[:, halves[h]], ALU.add)
+        for b, n in ((1, 6), (2, 7), (3, 4)):
+            still = quantise(b)
+            acc = bank(n, [P, S])
+            for h in range(2):
+                product(acc[:, halves[h]], still, h)
+            nc.vector.tensor_tensor(y[b][:], acc[:], bias_rows[:], ALU.add)
+
         margins = {}
 
-        def gather_margin(b, d):
-            if b == 0:
-                margins[b, d] = (first_pair if d < 2 else second_pair)[:, d % 2, :]
-            else:
-                tag = "third_factor" if (b, d) == (1, 0) else "margin%d_%d" % (b, d)
-                margin = keep.tile([P, U], F32, name="margin", tag=tag)
-                margins[b, d] = margin[:]
-            nc.vector.tensor_tensor(margins[b, d], y[b][:].indirect(pos_sb[d][:]), code_sb[d], ALU.mult)
+        def gather_margin(b, d, margin):
+            margins[b, d] = margin
+            nc.vector.tensor_tensor(margin, y[b][:].indirect(pos_sb[TURNED + d][:]), code_rows[d][:], ALU.mult)
 
-        grouped_last = keep.tile([P, PIECE, PACK], BF16, name="grouped_last", tag="word_table", align_bytes=64)
-        for b in (2, 3):
-            quantised.append(quantise(b, interleave(b, grouped_last[:, (b - 2) * P : (b - 1) * P, :])))
-            if b == 2:
-                first_pair = keep.tile([P, 2, U], F32, name="first_pair", tag="third_factor")
-                gather_margin(0, 0)
-                gather_margin(0, 1)
-        acc = bank(0, [P, S])
-        y[1] = placed.tile([P, S], F32, name="y1", offset=8192)
-        second_pair = placed.tile([P, 2, U], F32, name="second_pair", offset=8192 + 2048)
-        for h in range(2):
-            product(acc[:, halves[h]], quantised[1][0][:], quantised[1][1][:], x_code[h][:], x_scale[:, halves[h]])
-        nc.vector.tensor_tensor(y[1][:], acc[:], bias_spread[:], ALU.add)
+        gather_margin(0, 0, keep.tile([P, U], F32, name="margin0", tag="factor", align_bytes=64)[:])
+        gather_margin(1, 0, placed.tile([P, U], F32, name="margin1", offset=12288 + 2048, align_bytes=64)[:])
+        late = keep.tile([P, 3, U], F32, name="late", tag="bias_rows")
+        for b in range(3):
+            gather_margin(b, 1, late[:, b, :])
 
-        turned = {}
-        TURNED_AT = {2: 16384, 3: 16384 + 4096}
-        for b, n in ((2, 5), (3, 6)):
-            acc = bank(n, [P, S // P, P])
-            for c in range(S // P):
-                cols = slice(c * P, (c + 1) * P)
-                codes = x_code[c // 2][:, (c % 2) * P : (c % 2 + 1) * P]
-                product(acc[:, c, :], codes, x_scale[:, cols], quantised[b][0][:], quantised[b][1][:])
-            turned[b] = placed.tile([P, S // P, P], F32, name="y_turned%d" % b, offset=TURNED_AT[b])
-            for c in range(S // P):
-                column = bias_column[c // 2][:, c % 2 : c % 2 + 1]
-                nc.scalar.activation(turned[b][:, c, :], acc[:, c, :], ACT.Identity, bias=column)
-        for b in (2, 3):
-            upright = bank(b, [P, S])
-            for c in range(S // P):
-                nc.tensor.transpose(upright[:, c * P : (c + 1) * P], turned[b][:, c, :], ident[:])
-            nc.scalar.copy(y[b][:], upright[:])
+        def add_turned(sums, h, source, first, last):
+            nc.tensor.matmul(sums[:, h, :], source, ident[:], start=first, stop=last, is_transpose=True)
 
-        held = [(0, 1), (0, 2), (0, 3), (1, 1), (1, 2), (1, 3)]
+        terms = [(b, d) for b in range(BLOCKS) for d in range(TURNED)]
+        turned, sums = {}, {}
 
-        def add_hinge(b, d, first, last, sums):
-            if (b, d) not in margins:
-                gather_margin(b, d)
-            if (b, d) in held:
-                n = held.index((b, d))
-                at = TURNED_AT[2 + n // 3] + 32 + (n % 3 - 1) * 1024
-                hinge = placed.tile([P, U], F32, name="hinge%d_%d" % (b, d), offset=at)
-            else:
-                hinge = keep.tile([P, U], F32, name="hinge%d_%d" % (b, d))
-            nc.scalar.activation(hinge[:], margins[b, d], ACT.Relu, bias=1.0 / D)
+        def fetch(n):
+            b, d = terms[n]
+            fetched = keep.tile([P, U], F32, name="fetched%d" % n)
+            nc.scalar.activation(fetched[:], y[b][:].indirect(pos_sb[d][:]), ACT.Copy)
+            turned[n] = bank((0, 1, 5)[n % 3], [P, HALVES, P])
             for h in range(HALVES):
-                nc.tensor.matmul(
-                    sums[:, h, :],
-                    hinge[:, h * P : (h + 1) * P],
-                    ident[:],
-                    start=(d == first and h == 0),
-                    stop=(d == last and h == HALVES - 1),
-                    is_transpose=True,
+                nc.tensor.transpose(turned[n][:, h, :], fetched[:, h * P : (h + 1) * P], ident[:])
+
+        def hinge_at(n):
+            return 2048 + 1024 * n
+
+        def add_hinge(n):
+            b, d = terms[n]
+            if d == 0:
+                sums[b] = bank((2, 3, 6, 7)[b], [P, HALVES, P])
+            hinge = placed.tile([P, HALVES, P], F32, name="hinge%d" % n, offset=hinge_at(n))
+            for h in range(HALVES):
+                nc.scalar.activation(
+                    hinge[:, h, :],
+                    turned[n][:, h, :],
+                    ACT.Relu,
+                    bias=1.0 / D,
+                    scale=code_columns[:, HALVES * d + h : HALVES * d + h + 1],
                 )
+                add_turned(sums[b], h, hinge[:, h, :], d == 0 and h == 0, d == TURNED - 1 and h == HALVES - 1)
+            if d == 0:
+                for h in range(HALVES):
+                    add_turned(sums[b], h, share[:].to_broadcast([P, P]), False, False)
 
-        for b, terms, n_sums, n_back in ((0, (0, 1, 2, 3), 4, 1), (1, (1, 2, 3, 0), 7, 0), (2, (0, 1, 2, 3), 5, 6)):
-            sums = bank(n_sums, [P, HALVES, P])
-            for d in terms:
-                add_hinge(b, d, terms[0], terms[-1], sums)
-            summed = keep.tile([P, HALVES, P], F32, name="summed%d" % b)
-            nc.scalar.copy(summed[:], sums[:])
-            back = bank(n_back, [P, U])
-            for h in range(HALVES):
-                nc.tensor.transpose(back[:, h * P : (h + 1) * P], summed[:, h, :], ident[:])
+        def finish(b):
+            partial = keep.tile([P, U], F32, name="partial%d" % b)
             result = keep.tile([P, U], F32, name="result%d" % b)
-            nc.scalar.copy(result[:], back[:])
-            queue = nc.sync if b == 0 else nc.scalar
-            queue.dma_start(out[b * P : (b + 1) * P, :], result[:])
+            summed = sums[b][:].rearrange("p h r -> p (h r)")
+            pieces = [slice(0, U)] if b + 1 < BLOCKS else [slice(0, P), slice(P, U)]
+            for cols in pieces:
+                nc.vector.scalar_tensor_tensor(
+                    partial[:, cols], margins[b, 0][:, cols], -1.0 / D, summed[:, cols], ALU.max, ALU.add
+                )
+            if b + 1 < BLOCKS:
+                margin = placed.tile([P, U], F32, name="margin_behind%d" % b, offset=hinge_at(TURNED * b + 1))
+                gather_margin(*((2, 0), (3, 0), (3, 1))[b], margin[:])
+            for cols in pieces:
+                nc.vector.scalar_tensor_tensor(
+                    result[:, cols], margins[b, 1][:, cols], -1.0 / D, partial[:, cols], ALU.max, ALU.add
+                )
+            nc.sync.dma_start(out[b * P : (b + 1) * P, :], result[:])
 
-        last = BLOCKS - 1
-        for d in range(2):
-            gather_margin(last, d)
-        one_term = keep.tile([P, U], F32, name="one_term")
-        nc.vector.tensor_scalar(one_term[:], margins[last, 0], -1.0 / D, 1.0, ALU.max, ALU.add)
-        gather_margin(last, 2)
-        two_terms = keep.tile([P, U], F32, name="two_terms")
-        nc.vector.scalar_tensor_tensor(two_terms[:], margins[last, 1], -1.0 / D, one_term[:], ALU.max, ALU.add)
-        gather_margin(last, 3)
-        three_terms = [keep.tile([P, P], F32, name="three_terms%d" % h) for h in range(HALVES)]
-        for h in range(HALVES):
-            cols = slice(h * P, (h + 1) * P)
-            nc.vector.scalar_tensor_tensor(
-                three_terms[h][:], margins[last, 2][:, cols], -1.0 / D, two_terms[:, cols], ALU.max, ALU.add
-            )
-        result = keep.tile([P, U], F32, name="result%d" % last)
-        for h in range(HALVES):
-            cols = slice(h * P, (h + 1) * P)
-            nc.vector.scalar_tensor_tensor(
-                result[:, cols], margins[last, 3][:, cols], -1.0 / D, three_terms[h][:], ALU.max, ALU.add
-            )
-        nc.sync.dma_start(out[last * P : (last + 1) * P, :], result[:])
+        for n in range(AHEAD):
+            fetch(n)
+        for n in range(len(terms)):
+            add_hinge(n)
+            if n + AHEAD < len(terms):
+                fetch(n + AHEAD)
+            if terms[n][1] == TURNED - 1:
+                finish(terms[n][0])

@@ -21,10 +21,10 @@ PACK = 4
 BLOCKS = V // P
 HALVES = U // P
 HALF = S // 2
-TURNED = 2
-CHAINED = D - TURNED
-PIECES = TURNED * HALVES
-AHEAD = 2
+PIECES = D * HALVES
+AHEAD = 3
+CHAINED_BLOCKS = (1, 3)
+TURNED_BLOCKS = (0, 2)
 
 
 def tile_picked_yecoc_sum_p_kernel(
@@ -42,30 +42,27 @@ def tile_picked_yecoc_sum_p_kernel(
         scale_table = keep.tile([P, T], U8, name="scale_table")
         word_table = keep.tile([P, T], U32, name="word_table", align_bytes=64)
         bias_table = keep.tile([P, T], F32, name="bias_table")
-        code_rows = [keep.tile([P, U], F32, name="code_rows%d" % d) for d in range(CHAINED)]
+        code_first = keep.tile([P, U], F32, name="code_first")
+        code_rest = keep.tile([P, D - 1, U], F32, name="code_rest")
+        code_rows = [code_first[:]] + [code_rest[:, d, :] for d in range(D - 1)]
         code_pieces = keep.tile([P, P], F32, name="code_pieces")
         h_0 = keep.tile([P, PACK, P], F32, name="h_0")
-        h_1 = keep.tile([P, PACK, P], F32, name="h_1")
-        h_last = keep.tile([P, PACK, 2 * P], F32, name="h_last", tag="h_last")
+        h_1 = placed.tile([P, PACK, P], F32, name="h_1", offset=4096)
+        h_last = keep.tile([P, PACK, 2 * P], F32, name="h_last")
         h_blocks = [h_0[:], h_1[:], h_last[:, :, 0:P], h_last[:, :, P : 2 * P]]
         h_rows = hT.rearrange("(p j) w -> p j w", j=PACK)
-
-        def constant(name, value):
-            column = keep.tile([P, 1], F32, name=name, tag=name, align_bytes=64)
-            nc.vector.memset(column[:], value)
-            return column
 
         nc.gpsimd.memset(scale_table[:].bitcast(I32), 0)
         quarter_tile = placed.tile([P, 768], F32, name="quarter_tile", offset=12288, align_bytes=64)
         quarter = quarter_tile[:, 0:1]
         nc.vector.memset(quarter, 1.0 / D)
-        share = keep.tile([P, 1], F32, name="share")
-        nc.scalar.activation(share[:], quarter, ACT.Copy, scale=float(CHAINED))
+        factor = keep.tile([P, 1], F32, name="factor")
+        nc.scalar.activation(factor[:], quarter, ACT.Copy, scale=-1.0)
         sign_tile = placed.tile([P, 80], F32, name="sign_tile", offset=0, align_bytes=64)
         sign = sign_tile[:, 0:1]
         nc.vector.memset(sign, -1.0)
-        factor = constant("factor", -1.0 / D)
         nc.vector.memset(bias_table[0 : P - 1, :], 0.0)
+        nc.vector.memset(code_pieces[0 : P - PIECES, :], 0.0)
         nc.sync.dma_start(offs_sb[:], offs)
         nc.sync.dma_start(bias_table[P - 1 : P, :], bias[0:1, :])
         for q in range(4):
@@ -74,19 +71,17 @@ def tile_picked_yecoc_sum_p_kernel(
             )
         nc.sync.dma_start(h_0[:], h_rows[:, :, 0:P])
         nc.sync.dma_start(word_table[:].bitcast(I32), x_words[0].rearrange("p n t -> p (n t)").bitcast(I32))
-        nc.sync.dma_start(pos_sb[2][:], pos3)
-        nc.sync.dma_start(code_rows[0][:], code[TURNED])
-        nc.sync.dma_start(h_1[:], h_rows[:, :, P : 2 * P])
-        nc.sync.dma_start(h_last[:], h_rows[:, :, 2 * P : V])
         nc.sync.dma_start(pos_sb[0][:], pos1)
         nc.sync.dma_start(pos_sb[1][:], pos2)
-        nc.sync.dma_start(pos_sb[3][:], pos4)
-        nc.sync.dma_start(code_rows[1][:], code[TURNED + 1])
-
-        nc.gpsimd.memset(code_pieces[0 : P - PIECES, :], 0.0)
-        step = (P * U + U) // 2
-        spaced = code.rearrange("d p r -> (d p r)")[0 : PIECES * step].rearrange("(j x) -> j x", x=step)
-        nc.gpsimd.dma_start(code_pieces[P - PIECES : P, :], spaced[:, 0:P])
+        nc.sync.dma_start(h_1[:], h_rows[:, :, P : 2 * P])
+        nc.sync.dma_start(h_last[:], h_rows[:, :, 2 * P : V])
+        first, step = (D - 1) * U, (P * U - U) // 2
+        spaced = code.rearrange("d p r -> (d p r)")[first : first + PIECES * step].rearrange("(j x) -> j x", x=step)
+        nc.sync.dma_start(code_pieces[P - PIECES : P, :], spaced[:, 0:P])
+        nc.sync.dma_start(code_first[:], code[0])
+        for lst, pos in zip(pos_sb[2:], (pos3, pos4)):
+            nc.sync.dma_start(lst[:], pos)
+        nc.sync.dma_start(code_rest[:], code[1:D].rearrange("d p r -> p d r"))
 
         ident = keep.tile([P, P], F32, name="ident")
         make_identity(nc, ident[:])
@@ -111,7 +106,7 @@ def tile_picked_yecoc_sum_p_kernel(
                 grouped.rearrange("p (c i) t -> p c t i", i=4),
                 h_blocks[b].rearrange("p t (c i) -> p c t i", i=4),
                 ACT.Copy,
-                scale=factor[:] if b == 1 else -1.0 / D,
+                scale=factor[:],
             )
 
         for h in range(2):
@@ -136,7 +131,7 @@ def tile_picked_yecoc_sum_p_kernel(
             grouped.append(placed.tile([P, P, PACK], BF16, name="grouped%d" % b, offset=at, align_bytes=64)[:])
         for b in range(1, BLOCKS):
             interleave(b, grouped[b])
-        code_columns = keep.tile([P, PIECES], F32, name="code_columns", tag="h_last")
+        code_columns = keep.tile([P, PIECES], F32, name="code_columns")
         nc.scalar.copy(code_columns[:], turned_code[:, P - PIECES : P])
 
         x_scale = keep.tile([P, S], U8, name="x_scale", align_bytes=64)
@@ -149,7 +144,8 @@ def tile_picked_yecoc_sum_p_kernel(
             placed.tile([P, HALF], U32, name="x_code1", offset=2 * P, align_bytes=64),
         ]
 
-        y = [keep.tile([P, S], F32, name="y%d" % b) for b in range(BLOCKS)]
+        y = [placed.tile([P, S], F32, name="y0", offset=4096)]
+        y.extend(keep.tile([P, S], F32, name="y%d" % b) for b in range(1, BLOCKS))
 
         def quantise(b):
             codes = keep.tile([P, P], U32, name="h_code%d" % b, align_bytes=64)
@@ -176,33 +172,53 @@ def tile_picked_yecoc_sum_p_kernel(
         nc.vector.tensor_copy(x_code[0][:], word_table[:].indirect(offs_halves[0]))
         still = quantise(0)
         nc.vector.tensor_copy(x_code[1][:], word_table[:].indirect(offs_halves[1]))
+        first_scores = [bank(4 + h, [P, HALF]) for h in range(2)]
         for h in range(2):
-            acc = bank(4 + h, [P, HALF])
-            product(acc[:], still, h)
-            nc.vector.tensor_tensor(y[0][:, halves[h]], acc[:], bias_rows[:, halves[h]], ALU.add)
-        for b, n in ((1, 6), (2, 7), (3, 4)):
+            product(first_scores[h][:], still, h)
+        scores = {}
+
+        def multiply(b):
             still = quantise(b)
-            acc = bank(n, [P, S])
+            scores[b] = bank((6, 7, 4)[b - 1], [P, S])
             for h in range(2):
-                product(acc[:, halves[h]], still, h)
-            nc.vector.tensor_tensor(y[b][:], acc[:], bias_rows[:], ALU.add)
+                product(scores[b][:, halves[h]], still, h)
 
-        margins = {}
+        def add_bias(b):
+            nc.vector.tensor_tensor(y[b][:], scores[b][:], bias_rows[:], ALU.add)
 
-        def gather_margin(b, d, margin):
-            margins[b, d] = margin
-            nc.vector.tensor_tensor(margin, y[b][:].indirect(pos_sb[TURNED + d][:]), code_rows[d][:], ALU.mult)
+        margins, totals = {}, {}
 
-        gather_margin(0, 0, keep.tile([P, U], F32, name="margin0", tag="factor", align_bytes=64)[:])
-        gather_margin(1, 0, placed.tile([P, U], F32, name="margin1", offset=12288 + 2048, align_bytes=64)[:])
-        late = keep.tile([P, 3, U], F32, name="late", tag="bias_rows")
-        for b in range(3):
-            gather_margin(b, 1, late[:, b, :])
+        def gather(b, d):
+            margins[b, d] = keep.tile([P, U], F32, name="margin%d_%d" % (b, d))
+            nc.vector.tensor_tensor(margins[b, d][:], y[b][:].indirect(pos_sb[d][:]), code_rows[d], ALU.mult)
 
-        def add_turned(sums, h, source, first, last):
-            nc.tensor.matmul(sums[:, h, :], source, ident[:], start=first, stop=last, is_transpose=True)
+        def accumulate(b, d, pieces=(slice(0, U),)):
+            totals[b, d] = keep.tile([P, U], F32, name="total%d_%d" % (b, d))
+            for cols in pieces:
+                more, margin = totals[b, d][:, cols], margins[b, d][:, cols]
+                if d == 0:
+                    nc.vector.tensor_scalar(more, margin, -1.0 / D, 1.0, ALU.max, ALU.add)
+                else:
+                    nc.vector.scalar_tensor_tensor(more, margin, -1.0 / D, totals[b, d - 1][:, cols], ALU.max, ALU.add)
+            if d == D - 1:
+                nc.sync.dma_start(out[b * P : (b + 1) * P, :], totals[b, d][:])
 
-        terms = [(b, d) for b in range(BLOCKS) for d in range(TURNED)]
+        multiply(1)
+        for h in range(2):
+            nc.vector.tensor_tensor(y[0][:, halves[h]], first_scores[h][:], bias_rows[:, halves[h]], ALU.add)
+        multiply(2)
+        add_bias(1)
+        multiply(3)
+        chained = [(b, d) for b in CHAINED_BLOCKS for d in range(D)]
+        for n, term in enumerate(chained):
+            gather(*term)
+            if n > 0:
+                accumulate(*chained[n - 1], (slice(0, P), slice(P, U)) if n == len(chained) - 1 else (slice(0, U),))
+            if n < 2:
+                add_bias(2 + n)
+        accumulate(*chained[-1], (slice(0, P), slice(P, U)))
+
+        terms = [(b, d) for b in TURNED_BLOCKS for d in range(D)]
         turned, sums = {}, {}
 
         def fetch(n):
@@ -213,14 +229,11 @@ def tile_picked_yecoc_sum_p_kernel(
             for h in range(HALVES):
                 nc.tensor.transpose(turned[n][:, h, :], fetched[:, h * P : (h + 1) * P], ident[:])
 
-        def hinge_at(n):
-            return 2048 + 1024 * n
-
         def add_hinge(n):
             b, d = terms[n]
             if d == 0:
-                sums[b] = bank((2, 3, 6, 7)[b], [P, HALVES, P])
-            hinge = placed.tile([P, HALVES, P], F32, name="hinge%d" % n, offset=hinge_at(n))
+                sums[b] = bank((3, 2)[n // D], [P, HALVES, P])
+            hinge = keep.tile([P, HALVES, P], F32, name="hinge%d" % n)
             for h in range(HALVES):
                 nc.scalar.activation(
                     hinge[:, h, :],
@@ -229,28 +242,19 @@ def tile_picked_yecoc_sum_p_kernel(
                     bias=1.0 / D,
                     scale=code_columns[:, HALVES * d + h : HALVES * d + h + 1],
                 )
-                add_turned(sums[b], h, hinge[:, h, :], d == 0 and h == 0, d == TURNED - 1 and h == HALVES - 1)
-            if d == 0:
-                for h in range(HALVES):
-                    add_turned(sums[b], h, share[:].to_broadcast([P, P]), False, False)
+                nc.tensor.matmul(
+                    sums[b][:, h, :],
+                    hinge[:, h, :],
+                    ident[:],
+                    start=(d == 0 and h == 0),
+                    stop=(d == D - 1 and h == HALVES - 1),
+                    is_transpose=True,
+                )
 
         def finish(b):
-            partial = keep.tile([P, U], F32, name="partial%d" % b)
-            result = keep.tile([P, U], F32, name="result%d" % b)
-            summed = sums[b][:].rearrange("p h r -> p (h r)")
-            pieces = [slice(0, U)] if b + 1 < BLOCKS else [slice(0, P), slice(P, U)]
-            for cols in pieces:
-                nc.vector.scalar_tensor_tensor(
-                    partial[:, cols], margins[b, 0][:, cols], -1.0 / D, summed[:, cols], ALU.max, ALU.add
-                )
-            if b + 1 < BLOCKS:
-                margin = placed.tile([P, U], F32, name="margin_behind%d" % b, offset=hinge_at(TURNED * b + 1))
-                gather_margin(*((2, 0), (3, 0), (3, 1))[b], margin[:])
-            for cols in pieces:
-                nc.vector.scalar_tensor_tensor(
-                    result[:, cols], margins[b, 1][:, cols], -1.0 / D, partial[:, cols], ALU.max, ALU.add
-                )
-            nc.sync.dma_start(out[b * P : (b + 1) * P, :], result[:])
+            result = keep.tile([P, HALVES, P], F32, name="result%d" % b)
+            nc.scalar.copy(result[:], sums[b][:])
+            nc.scalar.dma_start(out[b * P : (b + 1) * P, :], result[:].rearrange("p h r -> p (h r)"))
 
         for n in range(AHEAD):
             fetch(n)
@@ -258,5 +262,5 @@ def tile_picked_yecoc_sum_p_kernel(
             add_hinge(n)
             if n + AHEAD < len(terms):
                 fetch(n + AHEAD)
-            if terms[n][1] == TURNED - 1:
+            if terms[n][1] == D - 1:
                 finish(terms[n][0])

@@ -46,19 +46,17 @@ def tile_picked_yecoc_sum_p_kernel(
         code_rest = keep.tile([P, D - 1, U], F32, name="code_rest")
         code_rows = [code_first[:]] + [code_rest[:, d, :] for d in range(D - 1)]
         code_pieces = keep.tile([P, P], F32, name="code_pieces")
-        h_0 = keep.tile([P, PACK, P], F32, name="h_0")
-        h_1 = placed.tile([P, PACK, P], F32, name="h_1", offset=4096)
-        h_last = keep.tile([P, PACK, 2 * P], F32, name="h_last")
-        h_blocks = [h_0[:], h_1[:], h_last[:, :, 0:P], h_last[:, :, P : 2 * P]]
+        h_pairs = [keep.tile([P, PACK, 2 * P], F32, name="h_pair", tag="h_pair%d" % n) for n in range(2)]
+        h_blocks = [h_pairs[b // 2][:, :, (b % 2) * P : (b % 2 + 1) * P] for b in range(BLOCKS)]
         h_rows = hT.rearrange("(p j) w -> p j w", j=PACK)
 
         nc.gpsimd.memset(scale_table[:].bitcast(I32), 0)
-        quarter_tile = placed.tile([P, 768], F32, name="quarter_tile", offset=12288, align_bytes=64)
+        quarter_tile = placed.tile([P, 512], F32, name="quarter_tile", offset=12288, align_bytes=64)
         quarter = quarter_tile[:, 0:1]
         nc.vector.memset(quarter, 1.0 / D)
         factor = keep.tile([P, 1], F32, name="factor")
         nc.scalar.activation(factor[:], quarter, ACT.Copy, scale=-1.0)
-        sign_tile = placed.tile([P, 80], F32, name="sign_tile", offset=0, align_bytes=64)
+        sign_tile = placed.tile([P, 576], F32, name="sign_tile", offset=0, align_bytes=64)
         sign = sign_tile[:, 0:1]
         nc.vector.memset(sign, -1.0)
         nc.vector.memset(bias_table[0 : P - 1, :], 0.0)
@@ -69,12 +67,11 @@ def tile_picked_yecoc_sum_p_kernel(
             nc.sync.dma_start(
                 scale_table[32 * q : 32 * q + 4, :].bitcast(I32), x_scales[0, 4 * q : 4 * q + 4, :].bitcast(I32)
             )
-        nc.sync.dma_start(h_0[:], h_rows[:, :, 0:P])
+        nc.sync.dma_start(h_pairs[0][:], h_rows[:, :, 0 : 2 * P])
         nc.sync.dma_start(word_table[:].bitcast(I32), x_words[0].rearrange("p n t -> p (n t)").bitcast(I32))
+        nc.sync.dma_start(h_pairs[1][:], h_rows[:, :, 2 * P : V])
         nc.sync.dma_start(pos_sb[0][:], pos1)
         nc.sync.dma_start(pos_sb[1][:], pos2)
-        nc.sync.dma_start(h_1[:], h_rows[:, :, P : 2 * P])
-        nc.sync.dma_start(h_last[:], h_rows[:, :, 2 * P : V])
         first, step = (D - 1) * U, (P * U - U) // 2
         spaced = code.rearrange("d p r -> (d p r)")[first : first + PIECES * step].rearrange("(j x) -> j x", x=step)
         nc.sync.dma_start(code_pieces[P - PIECES : P, :], spaced[:, 0:P])
@@ -124,33 +121,32 @@ def tile_picked_yecoc_sum_p_kernel(
             nc.scalar.activation(bias_rows[:, halves[h]], bias_spread[h][:], ACT.Copy, scale=quarter)
         turned_code = bank(2, [P, P])
         nc.tensor.transpose(turned_code[:], code_pieces[:], ident[:])
-        grouped_first = keep.tile([P, P, PACK], BF16, name="grouped_first", align_bytes=64)
-        grouped = [grouped_first[:]]
-        for b in range(1, BLOCKS):
-            at = 12288 + 1024 * (b - 1)
+        grouped = [keep.tile([P, P, PACK], BF16, name="grouped%d" % b, align_bytes=64)[:] for b in range(2)]
+        for b in range(2, BLOCKS):
+            at = 12288 + 1024 * (b - 2)
             grouped.append(placed.tile([P, P, PACK], BF16, name="grouped%d" % b, offset=at, align_bytes=64)[:])
-        for b in range(1, BLOCKS):
             interleave(b, grouped[b])
         code_columns = keep.tile([P, PIECES], F32, name="code_columns")
         nc.scalar.copy(code_columns[:], turned_code[:, P - PIECES : P])
 
         x_scale = keep.tile([P, S], U8, name="x_scale", align_bytes=64)
         nc.vector.tensor_copy(x_scale[:], scale_table[:].indirect(offs_sb[:]))
-        nc.vector.tensor_scalar_mul(
-            grouped[0].rearrange("p (c i) t -> p c t i", i=4), h_0[:].rearrange("p t (c i) -> p c t i", i=4), -1.0 / D
-        )
+        for b in range(2):
+            nc.vector.tensor_scalar_mul(
+                grouped[b].rearrange("p (c i) t -> p c t i", i=4),
+                h_blocks[b].rearrange("p t (c i) -> p c t i", i=4),
+                -1.0 / D,
+            )
         x_code = [
-            keep.tile([P, HALF], U32, name="x_code0", align_bytes=64),
-            placed.tile([P, HALF], U32, name="x_code1", offset=2 * P, align_bytes=64),
+            placed.tile([P, HALF], U32, name="x_code%d" % h, offset=256 + 1024 * h, align_bytes=64) for h in range(2)
         ]
 
-        y = [placed.tile([P, S], F32, name="y0", offset=4096)]
-        y.extend(keep.tile([P, S], F32, name="y%d" % b) for b in range(1, BLOCKS))
+        y = [keep.tile([P, S], F32, name="y%d" % b) for b in range(BLOCKS)]
 
         def quantise(b):
             codes = keep.tile([P, P], U32, name="h_code%d" % b, align_bytes=64)
-            if b == 0:
-                scales = placed.tile([P, P], U8, name="h_scale0", offset=0, align_bytes=64)
+            if b < 2:
+                scales = placed.tile([P, P], U8, name="h_scale%d" % b, offset=b * P, align_bytes=64)
             else:
                 scales = keep.tile([P, P], U8, name="h_scale%d" % b, align_bytes=64)
             nc.vector.quantize_mx(
@@ -169,17 +165,20 @@ def tile_picked_yecoc_sum_p_kernel(
                 stop=True,
             )
 
-        nc.vector.tensor_copy(x_code[0][:], word_table[:].indirect(offs_halves[0]))
-        still = quantise(0)
-        nc.vector.tensor_copy(x_code[1][:], word_table[:].indirect(offs_halves[1]))
-        first_scores = [bank(4 + h, [P, HALF]) for h in range(2)]
+        first_still = []
         for h in range(2):
-            product(first_scores[h][:], still, h)
+            first_still.append(quantise(h))
+            nc.vector.tensor_copy(x_code[h][:], word_table[:].indirect(offs_halves[h]))
+        for h in range(2):
+            for b in range(2):
+                acc = bank(4 + 2 * h + b, [P, HALF])
+                product(acc[:], first_still[b], h)
+                nc.vector.tensor_tensor(y[b][:, halves[h]], acc[:], bias_rows[:, halves[h]], ALU.add)
         scores = {}
 
         def multiply(b):
             still = quantise(b)
-            scores[b] = bank((6, 7, 4)[b - 1], [P, S])
+            scores[b] = bank((4, 6)[b - 2], [P, S])
             for h in range(2):
                 product(scores[b][:, halves[h]], still, h)
 
@@ -189,7 +188,8 @@ def tile_picked_yecoc_sum_p_kernel(
         margins, totals = {}, {}
 
         def gather(b, d):
-            margins[b, d] = keep.tile([P, U], F32, name="margin%d_%d" % (b, d))
+            tag = "h_pair1" if (b, d) == (CHAINED_BLOCKS[0], 0) else "margin%d_%d" % (b, d)
+            margins[b, d] = keep.tile([P, U], F32, name="margin", tag=tag)
             nc.vector.tensor_tensor(margins[b, d][:], y[b][:].indirect(pos_sb[d][:]), code_rows[d], ALU.mult)
 
         def accumulate(b, d, pieces=(slice(0, U),)):
@@ -203,19 +203,15 @@ def tile_picked_yecoc_sum_p_kernel(
             if d == D - 1:
                 nc.sync.dma_start(out[b * P : (b + 1) * P, :], totals[b, d][:])
 
-        multiply(1)
-        for h in range(2):
-            nc.vector.tensor_tensor(y[0][:, halves[h]], first_scores[h][:], bias_rows[:, halves[h]], ALU.add)
         multiply(2)
-        add_bias(1)
         multiply(3)
         chained = [(b, d) for b in CHAINED_BLOCKS for d in range(D)]
         for n, term in enumerate(chained):
             gather(*term)
+            if n in (1, 2):
+                add_bias(1 + n)
             if n > 0:
                 accumulate(*chained[n - 1], (slice(0, P), slice(P, U)) if n == len(chained) - 1 else (slice(0, U),))
-            if n < 2:
-                add_bias(2 + n)
         accumulate(*chained[-1], (slice(0, P), slice(P, U)))
 
         terms = [(b, d) for b in TURNED_BLOCKS for d in range(D)]

@@ -51,11 +51,11 @@ def tile_picked_yecoc_sum_p_kernel(
         h_rows = hT.rearrange("(p j) w -> p j w", j=PACK)
 
         nc.gpsimd.memset(scale_table[:].bitcast(I32), 0)
-        quarter_tile = placed.tile([P, 512], F32, name="quarter_tile", offset=12288, align_bytes=64)
-        quarter = quarter_tile[:, 0:1]
-        nc.vector.memset(quarter, 1.0 / D)
-        factor = keep.tile([P, 1], F32, name="factor")
-        nc.scalar.activation(factor[:], quarter, ACT.Copy, scale=-1.0)
+        quarter = keep.tile([P, 1], F32, name="quarter", tag="quarter", align_bytes=64)
+        nc.vector.memset(quarter[:], 1.0 / D)
+        factor_tile = placed.tile([P, 1056], F32, name="factor_tile", offset=8192, align_bytes=64)
+        factor = factor_tile[:, 0:1]
+        nc.scalar.activation(factor, quarter[:], ACT.Copy, scale=-1.0)
         sign_tile = placed.tile([P, 576], F32, name="sign_tile", offset=0, align_bytes=64)
         sign = sign_tile[:, 0:1]
         nc.vector.memset(sign, -1.0)
@@ -103,7 +103,7 @@ def tile_picked_yecoc_sum_p_kernel(
                 grouped.rearrange("p (c i) t -> p c t i", i=4),
                 h_blocks[b].rearrange("p t (c i) -> p c t i", i=4),
                 ACT.Copy,
-                scale=factor[:],
+                scale=factor,
             )
 
         for h in range(2):
@@ -116,17 +116,17 @@ def tile_picked_yecoc_sum_p_kernel(
                 )
             bias_spread.append(spread)
 
-        bias_rows = keep.tile([P, S], F32, name="bias_rows", tag="bias_rows")
+        grouped = [keep.tile([P, P, PACK], BF16, name="grouped%d" % b, align_bytes=64)[:] for b in range(2)]
+        bias_rows = keep.tile([P, S], F32, name="bias_rows")
         for h in range(2):
-            nc.scalar.activation(bias_rows[:, halves[h]], bias_spread[h][:], ACT.Copy, scale=quarter)
+            nc.scalar.activation(bias_rows[:, halves[h]], bias_spread[h][:], ACT.Copy, scale=quarter[:])
+        grouped.append(keep.tile([P, P, PACK], BF16, name="grouped2", tag="quarter", align_bytes=64)[:])
+        interleave(2, grouped[2])
+        grouped.append(keep.tile([P, P, PACK], BF16, name="grouped3", align_bytes=64)[:])
+        nc.gpsimd.tensor_scalar(grouped[3], h_blocks[3].rearrange("p t w -> p w t"), -1.0 / D, 0.0, ALU.mult, ALU.add)
         turned_code = bank(2, [P, P])
         nc.tensor.transpose(turned_code[:], code_pieces[:], ident[:])
-        grouped = [keep.tile([P, P, PACK], BF16, name="grouped%d" % b, align_bytes=64)[:] for b in range(2)]
-        for b in range(2, BLOCKS):
-            at = 12288 + 1024 * (b - 2)
-            grouped.append(placed.tile([P, P, PACK], BF16, name="grouped%d" % b, offset=at, align_bytes=64)[:])
-            interleave(b, grouped[b])
-        code_columns = keep.tile([P, PIECES], F32, name="code_columns")
+        code_columns = keep.tile([P, PIECES], F32, name="code_columns", tag="h_pair1")
         nc.scalar.copy(code_columns[:], turned_code[:, P - PIECES : P])
 
         x_scale = keep.tile([P, S], U8, name="x_scale", align_bytes=64)
@@ -141,12 +141,15 @@ def tile_picked_yecoc_sum_p_kernel(
             placed.tile([P, HALF], U32, name="x_code%d" % h, offset=256 + 1024 * h, align_bytes=64) for h in range(2)
         ]
 
-        y = [keep.tile([P, S], F32, name="y%d" % b) for b in range(BLOCKS)]
+        y = [placed.tile([P, S], F32, name="y%d" % b, offset=8192 + 2048 * b, align_bytes=64) for b in range(2)]
+        y.extend(keep.tile([P, S], F32, name="y%d" % b) for b in range(2, BLOCKS))
 
         def quantise(b):
             codes = keep.tile([P, P], U32, name="h_code%d" % b, align_bytes=64)
             if b < 2:
                 scales = placed.tile([P, P], U8, name="h_scale%d" % b, offset=b * P, align_bytes=64)
+            elif b == 3:
+                scales = placed.tile([P, P], U8, name="h_scale3", offset=8192 + 4096, align_bytes=64)
             else:
                 scales = keep.tile([P, P], U8, name="h_scale%d" % b, align_bytes=64)
             nc.vector.quantize_mx(
@@ -169,16 +172,11 @@ def tile_picked_yecoc_sum_p_kernel(
         for h in range(2):
             first_still.append(quantise(h))
             nc.vector.tensor_copy(x_code[h][:], word_table[:].indirect(offs_halves[h]))
-        for h in range(2):
-            for b in range(2):
-                acc = bank(4 + 2 * h + b, [P, HALF])
-                product(acc[:], first_still[b], h)
-                nc.vector.tensor_tensor(y[b][:, halves[h]], acc[:], bias_rows[:, halves[h]], ALU.add)
         scores = {}
 
         def multiply(b):
             still = quantise(b)
-            scores[b] = bank((4, 6)[b - 2], [P, S])
+            scores[b] = bank(4 + b, [P, S])
             for h in range(2):
                 product(scores[b][:, halves[h]], still, h)
 
@@ -188,8 +186,7 @@ def tile_picked_yecoc_sum_p_kernel(
         margins, totals = {}, {}
 
         def gather(b, d):
-            tag = "h_pair1" if (b, d) == (CHAINED_BLOCKS[0], 0) else "margin%d_%d" % (b, d)
-            margins[b, d] = keep.tile([P, U], F32, name="margin", tag=tag)
+            margins[b, d] = keep.tile([P, U], F32, name="margin%d_%d" % (b, d))
             nc.vector.tensor_tensor(margins[b, d][:], y[b][:].indirect(pos_sb[d][:]), code_rows[d], ALU.mult)
 
         def accumulate(b, d, pieces=(slice(0, U),)):
@@ -203,8 +200,15 @@ def tile_picked_yecoc_sum_p_kernel(
             if d == D - 1:
                 nc.sync.dma_start(out[b * P : (b + 1) * P, :], totals[b, d][:])
 
+        for b in range(2):
+            scores[b] = bank(4 + b, [P, S])
+        for h in range(2):
+            for b in range(2):
+                product(scores[b][:, halves[h]], first_still[b], h)
         multiply(2)
         multiply(3)
+        add_bias(0)
+        add_bias(1)
         chained = [(b, d) for b in CHAINED_BLOCKS for d in range(D)]
         for n, term in enumerate(chained):
             gather(*term)
@@ -221,7 +225,7 @@ def tile_picked_yecoc_sum_p_kernel(
             b, d = terms[n]
             fetched = keep.tile([P, U], F32, name="fetched%d" % n)
             nc.scalar.activation(fetched[:], y[b][:].indirect(pos_sb[d][:]), ACT.Copy)
-            turned[n] = bank((0, 1, 5)[n % 3], [P, HALVES, P])
+            turned[n] = bank((0, 1, 4)[n % 3], [P, HALVES, P])
             for h in range(HALVES):
                 nc.tensor.transpose(turned[n][:, h, :], fetched[:, h * P : (h + 1) * P], ident[:])
 

from contextlib import ExitStack

import concourse.mybir as mybir
from concourse.masks import make_identity

K, T, S, V, U, D = 512, 1024, 512, 512, 256, 4
FLOPS = 2 * K * V * S

F32 = mybir.dt.float32
BF16 = mybir.dt.bfloat16
I32 = mybir.dt.int32
U32 = mybir.dt.uint32
U16 = mybir.dt.uint16
U8 = mybir.dt.uint8
FP8X4 = mybir.dt.float8_e4m3fn_x4
ALU = mybir.AluOpType
ACT = mybir.ActivationFunctionType

P = 128
PACK = 4
BLOCKS = V // P
HALVES = U // P
HALF = S // 2
PIECES = D * HALVES
AHEAD = 3
CHAINED_BLOCKS = (1, 3)
TURNED_BLOCKS = (0, 2)


def tile_picked_yecoc_sum_p_kernel(
    tc, x_words, x_scales, hT, bias, code, offs, pos1, pos2, pos3, pos4, out
):
    nc = tc.nc
    with ExitStack() as ctx:
        keep = ctx.enter_context(tc.tile_pool(name="keep", bufs=1))
        psum = ctx.enter_context(tc.psum_pool(name="psum", bufs=1))

        placed = ctx.enter_context(tc.tile_pool(name="placed", bufs=1))

        offs_sb = keep.tile([P, S // 16], U16, name="offs_sb")
        pos_sb = [keep.tile([P, U // 16], U16, name="pos_sb%d" % d) for d in range(D)]
        scale_table = keep.tile([P, T], U8, name="scale_table")
        word_table = keep.tile([P, T], U32, name="word_table", align_bytes=64)
        bias_table = keep.tile([P, T], F32, name="bias_table")
        code_first = keep.tile([P, U], F32, name="code_first")
        code_rest = keep.tile([P, D - 1, U], F32, name="code_rest")
        code_rows = [code_first[:]] + [code_rest[:, d, :] for d in range(D - 1)]
        code_pieces = keep.tile([P, P], F32, name="code_pieces")
        h_pairs = [keep.tile([P, PACK, 2 * P], F32, name="h_pair", tag="h_pair%d" % n) for n in range(2)]
        h_blocks = [h_pairs[b // 2][:, :, (b % 2) * P : (b % 2 + 1) * P] for b in range(BLOCKS)]
        h_rows = hT.rearrange("(p j) w -> p j w", j=PACK)

        nc.gpsimd.memset(scale_table[:].bitcast(I32), 0)
        quarter = keep.tile([P, 1], F32, name="quarter", tag="quarter", align_bytes=64)
        nc.vector.memset(quarter[:], 1.0 / D)
        factor_tile = placed.tile([P, 1056], F32, name="factor_tile", offset=8192, align_bytes=64)
        factor = factor_tile[:, 0:1]
        nc.scalar.activation(factor, quarter[:], ACT.Copy, scale=-1.0)
        sign_tile = placed.tile([P, 576], F32, name="sign_tile", offset=0, align_bytes=64)
        sign = sign_tile[:, 0:1]
        nc.vector.memset(sign, -1.0)
        nc.vector.memset(bias_table[0 : P - 1, :], 0.0)
        nc.vector.memset(code_pieces[0 : P - PIECES, :], 0.0)
        nc.sync.dma_start(offs_sb[:], offs)
        nc.sync.dma_start(bias_table[P - 1 : P, :], bias[0:1, :])
        for q in range(4):
            nc.sync.dma_start(
                scale_table[32 * q : 32 * q + 4, :].bitcast(I32), x_scales[0, 4 * q : 4 * q + 4, :].bitcast(I32)
            )
        nc.sync.dma_start(h_pairs[0][:], h_rows[:, :, 0 : 2 * P])
        nc.sync.dma_start(word_table[:].bitcast(I32), x_words[0].rearrange("p n t -> p (n t)").bitcast(I32))
        nc.sync.dma_start(h_pairs[1][:], h_rows[:, :, 2 * P : V])
        nc.sync.dma_start(pos_sb[0][:], pos1)
        nc.sync.dma_start(pos_sb[1][:], pos2)
        first, step = (D - 1) * U, (P * U - U) // 2
        spaced = code.rearrange("d p r -> (d p r)")[first : first + PIECES * step].rearrange("(j x) -> j x", x=step)
        nc.sync.dma_start(code_pieces[P - PIECES : P, :], spaced[:, 0:P])
        nc.sync.dma_start(code_first[:], code[0])
        for lst, pos in zip(pos_sb[2:], (pos3, pos4)):
            nc.sync.dma_start(lst[:], pos)
        nc.sync.dma_start(code_rest[:], code[1:D].rearrange("d p r -> p d r"))

        ident = keep.tile([P, P], F32, name="ident")
        make_identity(nc, ident[:])

        halves = [slice(0, HALF), slice(HALF, S)]
        offs_halves = [offs_sb[:, 0 : S // 32], offs_sb[:, S // 32 : S // 16]]

        def bank(n, shape):
            return psum.tile(shape, F32, name="bank", tag="bank%d" % n)

        bias_spread = []
        turned_bias = []
        for h in range(2):
            picked = keep.tile([P, HALF], F32, name="picked%d" % h)
            nc.scalar.activation(picked[:], bias_table[:].indirect(offs_halves[h]), ACT.Copy)
            turned_bias.append(bank(h, [P, 2, P]))
            for c in range(2):
                nc.tensor.transpose(turned_bias[h][:, c, :], picked[:, c * P : (c + 1) * P], ident[:])

        def interleave(b, grouped):
            nc.scalar.activation(
                grouped.rearrange("p (c i) t -> p c t i", i=4),
                h_blocks[b].rearrange("p t (c i) -> p c t i", i=4),
                ACT.Copy,
                scale=factor,
            )

        for h in range(2):
            columns = keep.tile([P, 2], F32, name="bias_columns%d" % h)
            nc.scalar.activation(columns[:], turned_bias[h][:, :, P - 1], ACT.Copy, scale=sign)
            spread = bank(2 + h, [P, HALF])
            for c in range(2):
                nc.tensor.transpose(
                    spread[:, c * P : (c + 1) * P], columns[:, c : c + 1].to_broadcast([P, P]), ident[:]
                )
            bias_spread.append(spread)

        grouped = [keep.tile([P, P, PACK], BF16, name="grouped%d" % b, align_bytes=64)[:] for b in range(2)]
        bias_rows = keep.tile([P, S], F32, name="bias_rows")
        for h in range(2):
            nc.scalar.activation(bias_rows[:, halves[h]], bias_spread[h][:], ACT.Copy, scale=quarter[:])
        grouped.append(keep.tile([P, P, PACK], BF16, name="grouped2", tag="quarter", align_bytes=64)[:])
        interleave(2, grouped[2])
        grouped.append(keep.tile([P, P, PACK], BF16, name="grouped3", align_bytes=64)[:])
        nc.gpsimd.tensor_scalar(grouped[3], h_blocks[3].rearrange("p t w -> p w t"), -1.0 / D, 0.0, ALU.mult, ALU.add)
        turned_code = bank(2, [P, P])
        nc.tensor.transpose(turned_code[:], code_pieces[:], ident[:])
        code_columns = keep.tile([P, PIECES], F32, name="code_columns", tag="h_pair1")
        nc.scalar.copy(code_columns[:], turned_code[:, P - PIECES : P])

        x_scale = keep.tile([P, S], U8, name="x_scale", align_bytes=64)
        nc.vector.tensor_copy(x_scale[:], scale_table[:].indirect(offs_sb[:]))
        for b in range(2):
            nc.vector.tensor_scalar_mul(
                grouped[b].rearrange("p (c i) t -> p c t i", i=4),
                h_blocks[b].rearrange("p t (c i) -> p c t i", i=4),
                -1.0 / D,
            )
        x_code = [
            placed.tile([P, HALF], U32, name="x_code%d" % h, offset=256 + 1024 * h, align_bytes=64) for h in range(2)
        ]

        y = [placed.tile([P, S], F32, name="y%d" % b, offset=8192 + 2048 * b, align_bytes=64) for b in range(2)]
        y.extend(keep.tile([P, S], F32, name="y%d" % b) for b in range(2, BLOCKS))

        def quantise(b):
            codes = keep.tile([P, P], U32, name="h_code%d" % b, align_bytes=64)
            if b < 2:
                scales = placed.tile([P, P], U8, name="h_scale%d" % b, offset=b * P, align_bytes=64)
            elif b == 3:
                scales = placed.tile([P, P], U8, name="h_scale3", offset=8192 + 4096, align_bytes=64)
            else:
                scales = keep.tile([P, P], U8, name="h_scale%d" % b, align_bytes=64)
            nc.vector.quantize_mx(
                out=codes[:].bitcast(FP8X4), scales=scales[:], in_=grouped[b].rearrange("p w j -> p (w j)")
            )
            return codes, scales

        def product(acc, still, h):
            nc.tensor.matmul_mx(
                out=acc,
                lhsT=still[0][:].bitcast(FP8X4),
                lhsT_scale=still[1][:],
                rhs=x_code[h][:].bitcast(FP8X4),
                rhs_scale=x_scale[:, halves[h]],
                start=True,
                stop=True,
            )

        first_still = []
        for h in range(2):
            first_still.append(quantise(h))
            nc.vector.tensor_copy(x_code[h][:], word_table[:].indirect(offs_halves[h]))
        scores = {}

        def multiply(b):
            still = quantise(b)
            scores[b] = bank(4 + b, [P, S])
            for h in range(2):
                product(scores[b][:, halves[h]], still, h)

        def add_bias(b):
            nc.vector.tensor_tensor(y[b][:], scores[b][:], bias_rows[:], ALU.add)

        margins, totals = {}, {}

        def gather(b, d):
            margins[b, d] = keep.tile([P, U], F32, name="margin%d_%d" % (b, d))
            nc.vector.tensor_tensor(margins[b, d][:], y[b][:].indirect(pos_sb[d][:]), code_rows[d], ALU.mult)

        def accumulate(b, d, pieces=(slice(0, U),)):
            totals[b, d] = keep.tile([P, U], F32, name="total%d_%d" % (b, d))
            for cols in pieces:
                more, margin = totals[b, d][:, cols], margins[b, d][:, cols]
                if d == 0:
                    nc.vector.tensor_scalar(more, margin, -1.0 / D, 1.0, ALU.max, ALU.add)
                else:
                    nc.vector.scalar_tensor_tensor(more, margin, -1.0 / D, totals[b, d - 1][:, cols], ALU.max, ALU.add)
            if d == D - 1:
                nc.sync.dma_start(out[b * P : (b + 1) * P, :], totals[b, d][:])

        for b in range(2):
            scores[b] = bank(4 + b, [P, S])
        for h in range(2):
            for b in range(2):
                product(scores[b][:, halves[h]], first_still[b], h)
        multiply(2)
        multiply(3)
        add_bias(0)
        add_bias(1)
        chained = [(b, d) for b in CHAINED_BLOCKS for d in range(D)]
        for n, term in enumerate(chained):
            gather(*term)
            if n in (1, 2):
                add_bias(1 + n)
            if n > 0:
                accumulate(*chained[n - 1], (slice(0, P), slice(P, U)) if n == len(chained) - 1 else (slice(0, U),))
        accumulate(*chained[-1], (slice(0, P), slice(P, U)))

        terms = [(b, d) for b in TURNED_BLOCKS for d in range(D)]
        turned, sums = {}, {}

        def fetch(n):
            b, d = terms[n]
            fetched = keep.tile([P, U], F32, name="fetched%d" % n)
            nc.scalar.activation(fetched[:], y[b][:].indirect(pos_sb[d][:]), ACT.Copy)
            turned[n] = bank((0, 1, 4)[n % 3], [P, HALVES, P])
            for h in range(HALVES):
                nc.tensor.transpose(turned[n][:, h, :], fetched[:, h * P : (h + 1) * P], ident[:])

        def add_hinge(n):
            b, d = terms[n]
            if d == 0:
                sums[b] = bank((3, 2)[n // D], [P, HALVES, P])
            hinge = keep.tile([P, HALVES, P], F32, name="hinge%d" % n)
            for h in range(HALVES):
                nc.scalar.activation(
                    hinge[:, h, :],
                    turned[n][:, h, :],
                    ACT.Relu,
                    bias=1.0 / D,
                    scale=code_columns[:, HALVES * d + h : HALVES * d + h + 1],
                )
                nc.tensor.matmul(
                    sums[b][:, h, :],
                    hinge[:, h, :],
                    ident[:],
                    start=(d == 0 and h == 0),
                    stop=(d == D - 1 and h == HALVES - 1),
                    is_transpose=True,
                )

        def finish(b):
            result = keep.tile([P, HALVES, P], F32, name="result%d" % b)
            nc.scalar.copy(result[:], sums[b][:])
            nc.scalar.dma_start(out[b * P : (b + 1) * P, :], result[:].rearrange("p h r -> p (h r)"))

        for n in range(AHEAD):
            fetch(n)
        for n in range(len(terms)):
            add_hinge(n)
            if n + AHEAD < len(terms):
                fetch(n + AHEAD)
            if terms[n][1] == D - 1:
                finish(terms[n][0])
